import numpy as np
import ml_dtypes


def mxq(x, axis, fmt="e4m3"):
    dtype, down = {"e4m3": (ml_dtypes.float8_e4m3fn, 7), "e5m2": (ml_dtypes.float8_e5m2, 14)}[fmt]
    v = np.moveaxis(np.asarray(x, np.float32).astype(ml_dtypes.bfloat16).astype(np.float64), axis, -1)
    blocks = v.reshape(v.shape[:-1] + (-1, 32))
    amax = np.abs(blocks).max(-1, keepdims=True)
    byte = np.maximum(np.where(amax > 0, np.frexp(amax)[1] - 1 + 127, 0) - down, 1)
    scale = np.exp2(byte - 127.0)
    codes = (blocks / scale).astype(np.float32).astype(dtype).astype(np.float64)
    return np.moveaxis((codes * scale).reshape(v.shape), -1, axis)


WIDE = False


def mx_kscale(k):
    if not WIDE:
        return np.ones(k)
    levels = np.array([10, -10, 5, -5, 0])
    if k % 512:
        return np.exp2(np.random.permutation(np.resize(levels, k // 32))).repeat(32)
    a = np.empty((k // 512, 16))
    for p in range(k // 512):
        a[p, :8] = np.random.permutation(np.resize(levels, 8))
        for g in range(8):
            far = levels[np.abs(levels - a[p, g]) >= 10]
            a[p, g + 8] = far[np.random.randint(len(far))]
    return np.exp2(a.ravel()).repeat(32)


def f64(x):
    return np.asarray(x).astype(np.float64)


def striped(idx):
    return np.tile(idx.reshape(-1, 16).T, (8, 1)).astype(np.uint16)


def unstriped(offs):
    return offs[:16].T.reshape(-1).astype(np.int64)


E2M1 = np.array([0.0, 0.5, 1.0, 1.5, 2.0, 3.0, 4.0, 6.0, -0.0, -0.5, -1.0, -1.5, -2.0, -3.0, -4.0, -6.0])


def pack_weight(w, fmt):
    k, n = w.shape
    w = f64(np.asarray(w, np.float32).astype(ml_dtypes.bfloat16)).reshape(k // 32, 32, n)
    amax = np.abs(w).max(1)
    if fmt == "e4m3":
        byte = np.frexp(amax)[1] - 1 + 127 - 7
    else:
        mant, ex = np.frexp(amax / 6.0)
        byte = np.where(mant > 0.5, ex, ex - 1) + 127
    byte = np.clip(np.where(amax > 0, byte, 1), 1, 254)
    scaled = (w * np.exp2(127.0 - byte)[:, None, :]).reshape(k, n).astype(np.float32)
    by_word = np.ascontiguousarray(scaled.reshape(k // 512, 128, 4, n).transpose(0, 1, 3, 2))
    if fmt == "e4m3":
        words = by_word.astype(ml_dtypes.float8_e4m3fn).view(np.uint8)
    else:
        c = by_word.astype(ml_dtypes.float4_e2m1fn).view(np.uint8) & 0xF
        words = (c[..., 0::2] | (c[..., 1::2] << 4)).reshape(k // 512, 128, 2 * n)
    return np.ascontiguousarray(words), np.ascontiguousarray(byte.astype(np.uint8).reshape(k // 512, 16, n))


def unpack_weight(words, scales, fmt):
    g, _, n = scales.shape
    words = np.ascontiguousarray(words).reshape(g, 128, n, -1)
    if fmt == "e4m3":
        vals = words.view(ml_dtypes.float8_e4m3fn).astype(np.float64)
    else:
        nib = np.empty((g, 128, n, 4), np.uint8)
        nib[..., 0::2] = words & 0xF
        nib[..., 1::2] = words >> 4
        vals = E2M1[nib]
    vals = vals * np.repeat(np.exp2(scales.astype(np.float64) - 127.0), 8, axis=1)[..., None]
    return vals.transpose(0, 1, 3, 2).reshape(g * 512, n)


def gelu(v):
    return 0.5 * v * (1.0 + np.tanh(np.sqrt(2.0 / np.pi) * (v + 0.044715 * v**3)))


K, K2, H, N, T, S, T2 = 1024, 512, 512, 256, 2048, 1024, 2048

def setup_inputs():
    n = np.random.standard_normal
    s, s2, u = mx_kscale(K)[:, None], mx_kscale(K2)[:, None], mx_kscale(H)[:, None]
    perm = np.random.permutation(T2)
    tab_words, tab_scales = pack_weight(n((K, T)) * s, "e4m3")
    tab2_words, tab2_scales = pack_weight(n((K2, T)) * s2, "e4m3")
    w2_words, w2_scales = pack_weight(0.5 * n((K2, H)) / np.sqrt(K2) / s2, "e2m1")
    wb_words, wb_scales = pack_weight(n((H, N)) / np.sqrt(H) / u, "e4m3")
    return {
        "tab_words": tab_words, "tab_scales": tab_scales,
        "tab2_words": tab2_words, "tab2_scales": tab2_scales,
        "offs": striped(np.random.permutation(T)[:S]),
        "offs2": striped(np.random.permutation(T)[:S]),
        "offs3": striped(perm[:S]), "offs4": striped(perm[S:]),
        "w1": (n((K, H)) / np.sqrt(K) / s * u.T).astype(np.float32),
        "w2_words": w2_words, "w2_scales": w2_scales,
        "tint": (np.exp(0.3 * n(H)) * u[:, 0]).astype(np.float32),
        "wg1": np.exp(0.3 * n((128, S))).astype(np.float32),
        "wg2": np.exp(0.3 * n((128, S))).astype(np.float32),
        "hist": (0.5 * n((H, T2)) * u).astype(np.float32),
        "wa": (n((H, N)) / np.sqrt(H) / u).astype(np.float32),
        "wb_words": wb_words, "wb_scales": wb_scales,
    }

def reference(tab_words, tab_scales, tab2_words, tab2_scales, offs, offs2, offs3, offs4, w1, w2_words, w2_scales, tint, wg1, wg2, hist, wa, wb_words, wb_scales):
    v = unpack_weight(tab_words, tab_scales, "e4m3")[:, unstriped(offs)]
    v2 = unpack_weight(tab2_words, tab2_scales, "e4m3")[:, unstriped(offs2)]
    h1 = np.maximum(mxq(f64(w1), 0, "e4m3").T @ v, 0.0)
    h2 = f64(tint)[:, None] * np.exp(unpack_weight(w2_words, w2_scales, "e2m1").T @ v2)
    page = np.zeros((H, T2))
    page[:, unstriped(offs3)] = np.tile(f64(wg1), (H // 128, 1)) * h1
    page[:, unstriped(offs4)] = np.tile(f64(wg2), (H // 128, 1)) * h2
    z = mxq(page + f64(hist), 0, "e4m3")
    light = mxq(f64(wa), 0, "e4m3").T @ z
    vis = unpack_weight(wb_words, wb_scales, "e4m3").T @ z
    return light / (1.0 + np.exp(-vis))

@@ -1,0 +1,258 @@
+from contextlib import ExitStack
+
+import concourse.mybir as mybir
+from concourse.masks import make_identity
+
+K, K2, H, N, T, S, T2 = 1024, 512, 512, 256, 2048, 1024, 2048
+FLOPS = 2 * (K * H * S + K2 * H * S + 2 * H * N * T2)
+
+F32 = mybir.dt.float32
+BF16 = mybir.dt.bfloat16
+I32 = mybir.dt.int32
+U32 = mybir.dt.uint32
+U16 = mybir.dt.uint16
+U8 = mybir.dt.uint8
+FP8X4 = mybir.dt.float8_e4m3fn_x4
+FP4X4 = mybir.dt.float4_e2m1fn_x4
+ACT = mybir.ActivationFunctionType
+MULT = mybir.AluOpType.mult
+ADD = mybir.AluOpType.add
+
+P = 128
+PACK = 4
+QUAD = 32
+BANK = 512
+AL = 64
+
+
+def tile_list_woven_probe_lighting_kernel(
+    tc, tab_words, tab_scales, tab2_words, tab2_scales, offs, offs2, offs3, offs4,
+    w1, w2_words, w2_scales, tint, wg1, wg2, hist, wa, wb_words, wb_scales, out,
+):
+    nc = tc.nc
+    with ExitStack() as ctx:
+        lists = ctx.enter_context(tc.tile_pool(name="lists", bufs=1))
+        sb = ctx.enter_context(tc.tile_pool(name="sb", bufs=1))
+        ps = ctx.enter_context(tc.psum_pool(name="ps", bufs=4))
+
+        def new_tile(shape, dtype, name, tag=None, bufs=1):
+            return sb.tile(shape, dtype, name=name, tag=tag or name, bufs=bufs, align_bytes=AL)
+
+        def load_list(src, name):
+            dst = lists.tile([P, S // 16], U16, name=name)
+            nc.sync.dma_start(dst[:], src)
+            return dst
+
+        def load_words(src, name):
+            cols = src.shape[1]
+            dst = new_tile([P, cols], U32, name)
+            nc.sync.dma_start(dst[:].bitcast(I32), src.rearrange("p n i -> p (n i)").bitcast(I32))
+            return dst
+
+        def load_scales(src, name, clear, queue):
+            passes, cols = src.shape[0], src.shape[2]
+            dst = new_tile([P, cols], U8, name)
+            clear.memset(dst[:].bitcast(I32), 0)
+            for q in range(4):
+                queue.dma_start(
+                    dst[QUAD * q : QUAD * q + 4 * passes, :].bitcast(I32),
+                    src[:, 4 * q : 4 * q + 4, :].bitcast(I32),
+                )
+            return dst
+
+        def load_wg(src, t0, t1, name, tag=None):
+            dst = new_tile([P, t1 - t0, S], F32, name, tag)
+            rows = src.rearrange("(q t) j -> q t j", t=PACK)
+            for g in range(4):
+                nc.sync.dma_start(dst[QUAD * g : QUAD * (g + 1), :, :], rows[:, t0:t1, :])
+            return [dst[:, t, :] for t in range(t1 - t0)]
+
+        o2 = load_list(offs2, "o2")
+        tab2s = load_scales(tab2_scales, "tab2s", nc.gpsimd, nc.sync)
+        w2raw = new_tile([P, 2 * H], U8, "w2raw")
+        nc.sync.dma_start(w2raw[:].bitcast(I32), w2_words[0].bitcast(I32))
+        tab2w = load_words(tab2_words[0], "tab2w")
+        w2sraw = load_scales(w2_scales, "w2sraw", nc.gpsimd, nc.sync)
+        tint_sb = new_tile([P, PACK], F32, "tint_sb")
+        nc.sync.dma_start(tint_sb[:], tint.rearrange("(p t) -> p t", t=PACK))
+        o1 = load_list(offs, "o1")
+        tabs = load_scales(tab_scales, "tabs", nc.gpsimd, nc.sync)
+        tabw = [load_words(tab_words[0], "tabw0")]
+        o4 = load_list(offs4, "o4")
+        wg2_sb = load_wg(wg2, 0, 1, "wg2a")
+        w1raw = []
+        for a in range(2):
+            if a == 1:
+                tabw.append(load_words(tab_words[1], "tabw1"))
+            raw = new_tile([P, PACK, H], F32, f"w1raw{a}")
+            nc.sync.dma_start(raw[:], w1[512 * a : 512 * (a + 1), :].rearrange("(p j) c -> p j c", j=PACK))
+            w1raw.append(raw)
+        wg2_sb = wg2_sb + load_wg(wg2, 1, 3, "wg2b")
+        o3 = load_list(offs3, "o3")
+        wg1_sb = load_wg(wg1, 0, 2, "wg1a") + load_wg(wg1, 2, 4, "wg1b")
+        waraw = new_tile([P, PACK, N], F32, "waraw")
+        nc.sync.dma_start(waraw[:], wa.rearrange("(p j) c -> p j c", j=PACK))
+        wbw = load_words(wb_words[0], "wbw")
+        wbs = load_scales(wb_scales, "wbs", nc.gpsimd, nc.sync)
+        ident = new_tile([P, P], F32, "ident")
+        make_identity(nc, ident[:])
+
+        w2c = new_tile([P, 2 * H], U8, "w2c")
+        w2s = new_tile([P, H], U8, "w2s")
+        nc.vector.tensor_copy(
+            w2c[:].bitcast(U16).rearrange("p (t m) -> p t m", t=PACK),
+            w2raw[:].bitcast(U16).rearrange("p (m t) -> p t m", t=PACK),
+        )
+        nc.vector.tensor_copy(
+            w2s[:].rearrange("p (t m) -> p t m", t=PACK),
+            w2sraw[:].rearrange("p (m t) -> p t m", t=PACK),
+        )
+
+        g2s = new_tile([P, S], U8, "g2s")
+        nc.vector.tensor_copy(g2s[:], tab2s[:].indirect(o2[:]))
+        g2w = new_tile([P, S], U32, "g2w")
+        for b in range(2):
+            nc.vector.tensor_copy(g2w[:, BANK * b : BANK * (b + 1)], tab2w[:].indirect(o2[:, 32 * b : 32 * (b + 1)]))
+        g1s = new_tile([P, S], U8, "g1s")
+        nc.vector.tensor_copy(g1s[:], tabs[:].indirect(o1[:]))
+
+        page = [new_tile([P, T2], F32, f"page{t}") for t in range(PACK)]
+        h1 = [new_tile([P, S], F32, f"h1_{t}") for t in range(PACK)]
+        h2_tags = ["h2_0", "w1raw1", "w1raw0", "w1b"]
+        h2 = []
+
+        def glossy(t):
+            h2.append(new_tile([P, S], F32, f"h2_{t}", h2_tags[t]))
+            for b in range(2):
+                cols = slice(BANK * b, BANK * (b + 1))
+                acc = ps.tile([P, BANK], F32, name="acc", tag="mm")
+                nc.tensor.matmul_mx(
+                    acc[:],
+                    lhsT=w2c[:, 2 * P * t : 2 * P * (t + 1)].bitcast(FP4X4),
+                    lhsT_scale=w2s[:, P * t : P * (t + 1)],
+                    rhs=g2w[:, cols].bitcast(FP8X4),
+                    rhs_scale=g2s[:, cols],
+                    start=True, stop=True,
+                )
+                nc.scalar.activation(h2[t][:, cols], acc[:], ACT.Exp)
+            for b in range(2):
+                cols = slice(BANK * b, BANK * (b + 1))
+                nc.scalar.activation(h2[t][:, cols], h2[t][:, cols], ACT.Copy, scale=tint_sb[:, t : t + 1])
+
+        def scatter(t, places, h, wg):
+            nc.vector.tensor_tensor(page[t][:].indirect(places[:]), h[t][:], wg[t], MULT)
+
+        glossy(0)
+        scatter(0, o4, h2, wg2_sb)
+
+        g1w = new_tile([P, 2, S], U32, "g1w")
+        for a in range(2):
+            nc.vector.tensor_copy(g1w[:, a, :], tabw[a][:].indirect(o1[:]))
+
+        w1b = new_tile([P, PACK, 2, P, PACK], BF16, "w1b")
+        for a in range(2):
+            nc.scalar.copy(
+                w1b[:, :, a, :, :].rearrange("p t m j -> p m t j"),
+                w1raw[a][:].rearrange("p j (m t) -> p m t j", t=PACK),
+            )
+        w1c = new_tile([P, PACK * 2 * P], U32, "w1c")
+        w1s = new_tile([P, PACK * 2 * P], U8, "w1s")
+        nc.vector.quantize_mx(w1c[:].bitcast(FP8X4), w1s[:], w1b[:].rearrange("p t a m j -> p (t a m j)"))
+
+        for t in range(1, PACK):
+            glossy(t)
+        warm = new_tile([P, 1], F32, "warm")
+        nc.scalar.activation(warm[:], h2[PACK - 1][:, S - 1 : S], ACT.Sigmoid)
+        for t in range(1, PACK - 1):
+            scatter(t, o4, h2, wg2_sb)
+
+        for t in range(PACK):
+            for b in range(2):
+                cols = slice(BANK * b, BANK * (b + 1))
+                acc = ps.tile([P, BANK], F32, name="acc", tag="mm")
+                for a in range(2):
+                    wcols = slice(P * (2 * t + a), P * (2 * t + a + 1))
+                    nc.tensor.matmul_mx(
+                        acc[:],
+                        lhsT=w1c[:, wcols].bitcast(FP8X4),
+                        lhsT_scale=w1s[:, wcols],
+                        rhs=g1w[:, a, cols].bitcast(FP8X4),
+                        rhs_scale=g1s[4 * a : P, cols],
+                        start=(a == 0), stop=(a == 1),
+                    )
+                nc.scalar.activation(h1[t][:, cols], acc[:], ACT.Relu)
+
+        wab = new_tile([P, N, PACK], BF16, "wab")
+        nc.scalar.copy(wab[:], waraw[:].rearrange("p j n -> p n j"))
+        wac = new_tile([P, N], U32, "wac")
+        was = new_tile([P, N], U8, "was")
+        nc.vector.quantize_mx(wac[:].bitcast(FP8X4), was[:], wab[:].rearrange("p n j -> p (n j)"))
+
+        hist_rows = hist.rearrange("(p t) m -> t p m", t=PACK)
+        hist_sb = []
+        for t, tag in enumerate(("g1w", "tab2w", "tabw0")):
+            rows = new_tile([P, T2], F32, f"hist{t}", tag)
+            nc.sync.dma_start(rows[:], hist_rows[t])
+            hist_sb.append(rows)
+
+        for t in range(PACK - 1):
+            scatter(t, o3, h1, wg1_sb)
+        wg2_sb = wg2_sb + load_wg(wg2, 3, 4, "wg2c", "wg1a")
+        scatter(PACK - 1, o4, h2, wg2_sb)
+        scatter(PACK - 1, o3, h1, wg1_sb)
+
+        chunks = T2 // BANK
+        blocks = BANK // P
+        zt = [new_tile([P, blocks, P, 2], BF16, f"zt{c}") for c in range(chunks)]
+        pairs = [new_tile([P, 2, BANK], F32, f"pairs{c}") for c in range(chunks)]
+
+        def add_turned(t, c):
+            bank = ps.tile([P, blocks, P], F32, name="bank", tag="tr")
+            for blk in range(blocks):
+                cols = slice(BANK * c + P * blk, BANK * c + P * (blk + 1))
+                nc.tensor.matmul(bank[:, blk, :], lhsT=hist_sb[t][:, cols], rhs=ident[:], is_transpose=True, start=True, stop=False)
+                nc.tensor.matmul(bank[:, blk, :], lhsT=page[t][:, cols], rhs=ident[:], is_transpose=True, start=False, stop=True)
+            nc.scalar.copy(zt[c][:, :, :, t % 2], bank[:])
+
+        def turn_back(u, c):
+            bank = ps.tile([P, blocks, P], F32, name="bank", tag="tr")
+            words = zt[c][:].rearrange("m b p e -> m (b p e)").bitcast(F32)
+            for blk in range(blocks):
+                nc.tensor.transpose(bank[:, blk, :], words[:, P * blk : P * (blk + 1)], ident[:])
+            nc.scalar.copy(pairs[c][:, u, :], bank[:].rearrange("p b m -> p (b m)"))
+
+        for c in range(chunks):
+            add_turned(0, c)
+        for t in (1, 2):
+            for c in range(chunks):
+                add_turned(t, c)
+            for c in range(chunks):
+                turn_back(t - 1, c)
+        rows = new_tile([P, T2], F32, "hist3", "tabw0")
+        nc.sync.dma_start(rows[:], hist_rows[PACK - 1])
+        hist_sb.append(rows)
+
+        free_tags = h2_tags + [f"h1_{t}" for t in range(PACK)]
+        for c in range(chunks):
+            cols = slice(BANK * c, BANK * (c + 1))
+            halves = pairs[c][:, 1, :].bitcast(BF16).rearrange("p (m e) -> p m e", e=2)
+            nc.vector.tensor_tensor(halves[:, :, 1], page[PACK - 1][:, cols], hist_sb[PACK - 1][:, cols], ADD)
+            zb = new_tile([P, BANK, 2], F32, "zb", bufs=3)
+            nc.scalar.copy(zb[:], pairs[c][:].rearrange("p u m -> p m u"))
+            zc = new_tile([P, BANK], U32, "zc", bufs=3)
+            zs = new_tile([P, BANK], U8, "zs", bufs=3)
+            nc.vector.quantize_mx(zc[:].bitcast(FP8X4), zs[:], zb[:].rearrange("p m u -> p (m u)").bitcast(BF16))
+            for n in range(N // P):
+                rows = slice(P * n, P * (n + 1))
+                vis = ps.tile([P, BANK], F32, name="vis", tag="mm")
+                light = ps.tile([P, BANK], F32, name="light", tag="tr")
+                for acc, wc, ws in ((vis, wbw, wbs), (light, wac, was)):
+                    nc.tensor.matmul_mx(
+                        acc[:], lhsT=wc[:, rows].bitcast(FP8X4), lhsT_scale=ws[:, rows],
+                        rhs=zc[:].bitcast(FP8X4), rhs_scale=zs[:], start=True, stop=True,
+                    )
+                gate = new_tile([P, BANK], F32, "gate", bufs=3)
+                nc.scalar.activation(gate[:], vis[:], ACT.Sigmoid)
+                res = new_tile([P, BANK], F32, "res", free_tags[2 * c + n])
+                nc.vector.tensor_tensor(res[:], light[:], gate[:], MULT)
+                nc.sync.dma_start(out[rows, cols], res[:])

@@ -69,21 +69,19 @@ def tile_list_woven_probe_lighting_kernel(
 
         o2 = load_list(offs2, "o2")
         tab2s = load_scales(tab2_scales, "tab2s", nc.gpsimd, nc.sync)
+        o1 = load_list(offs, "o1")
         w2raw = new_tile([P, 2 * H], U8, "w2raw")
         nc.sync.dma_start(w2raw[:].bitcast(I32), w2_words[0].bitcast(I32))
         tab2w = load_words(tab2_words[0], "tab2w")
+        tabs = load_scales(tab_scales, "tabs", nc.gpsimd, nc.sync)
         w2sraw = load_scales(w2_scales, "w2sraw", nc.gpsimd, nc.sync)
+        tabw = [load_words(tab_words[a], f"tabw{a}") for a in range(2)]
         tint_sb = new_tile([P, PACK], F32, "tint_sb")
         nc.sync.dma_start(tint_sb[:], tint.rearrange("(p t) -> p t", t=PACK))
-        o1 = load_list(offs, "o1")
-        tabs = load_scales(tab_scales, "tabs", nc.gpsimd, nc.sync)
-        tabw = [load_words(tab_words[0], "tabw0")]
         o4 = load_list(offs4, "o4")
         wg2_sb = load_wg(wg2, 0, 1, "wg2a")
         w1raw = []
         for a in range(2):
-            if a == 1:
-                tabw.append(load_words(tab_words[1], "tabw1"))
             raw = new_tile([P, PACK, H], F32, f"w1raw{a}")
             nc.sync.dma_start(raw[:], w1[512 * a : 512 * (a + 1), :].rearrange("(p j) c -> p j c", j=PACK))
             w1raw.append(raw)
@@ -143,11 +141,10 @@ def tile_list_woven_probe_lighting_kernel(
             nc.vector.tensor_tensor(page[t][:].indirect(places[:]), h[t][:], wg[t], MULT)
 
         glossy(0)
-        scatter(0, o4, h2, wg2_sb)
-
         g1w = new_tile([P, 2, S], U32, "g1w")
         for a in range(2):
             nc.vector.tensor_copy(g1w[:, a, :], tabw[a][:].indirect(o1[:]))
+        scatter(0, o4, h2, wg2_sb)
 
         w1b = new_tile([P, PACK, 2, P, PACK], BF16, "w1b")
         for a in range(2):

@@ -33,6 +33,7 @@ def tile_list_woven_probe_lighting_kernel(
     with ExitStack() as ctx:
         lists = ctx.enter_context(tc.tile_pool(name="lists", bufs=1))
         sb = ctx.enter_context(tc.tile_pool(name="sb", bufs=1))
+        shared = ctx.enter_context(tc.tile_pool(name="shared", bufs=1))
         ps = ctx.enter_context(tc.psum_pool(name="ps", bufs=4))
 
         def new_tile(shape, dtype, name, tag=None, bufs=1):
@@ -60,12 +61,12 @@ def tile_list_woven_probe_lighting_kernel(
                 )
             return dst
 
-        def load_wg(src, t0, t1, name, tag=None):
-            dst = new_tile([P, t1 - t0, S], F32, name, tag)
-            rows = src.rearrange("(q t) j -> q t j", t=PACK)
-            for g in range(4):
-                nc.sync.dma_start(dst[QUAD * g : QUAD * (g + 1), :, :], rows[:, t0:t1, :])
-            return [dst[:, t, :] for t in range(t1 - t0)]
+        def load_wg(src, t, name, tag=None):
+            dst = new_tile([P, S], F32, name, tag)
+            rows = src.rearrange("(q t) j -> t q j", t=PACK)
+            for g in (0, 2, 1, 3):
+                nc.sync.dma_start(dst[QUAD * g : QUAD * (g + 1), :], rows[t])
+            return dst
 
         o2 = load_list(offs2, "o2")
         tab2s = load_scales(tab2_scales, "tab2s", nc.gpsimd, nc.sync)
@@ -79,21 +80,21 @@ def tile_list_woven_probe_lighting_kernel(
         tint_sb = new_tile([P, PACK], F32, "tint_sb")
         nc.sync.dma_start(tint_sb[:], tint.rearrange("(p t) -> p t", t=PACK))
         o4 = load_list(offs4, "o4")
-        wg2_sb = load_wg(wg2, 0, 1, "wg2a")
+        wg2_sb = [load_wg(wg2, 0, "wg2_0")]
         w1raw = []
         for a in range(2):
             raw = new_tile([P, PACK, H], F32, f"w1raw{a}")
             nc.sync.dma_start(raw[:], w1[512 * a : 512 * (a + 1), :].rearrange("(p j) c -> p j c", j=PACK))
             w1raw.append(raw)
-        wg2_sb = wg2_sb + load_wg(wg2, 1, 3, "wg2b")
+        wg2_sb.append(load_wg(wg2, 1, "wg2_1"))
         o3 = load_list(offs3, "o3")
-        wg1_sb = load_wg(wg1, 0, 2, "wg1a") + load_wg(wg1, 2, 4, "wg1b")
+        wg1_sb = [load_wg(wg1, t, f"wg1_{t}") for t in range(PACK - 1)]
         waraw = new_tile([P, PACK, N], F32, "waraw")
         nc.sync.dma_start(waraw[:], wa.rearrange("(p j) c -> p j c", j=PACK))
         wbw = load_words(wb_words[0], "wbw")
         wbs = load_scales(wb_scales, "wbs", nc.gpsimd, nc.sync)
-        ident = new_tile([P, P], F32, "ident")
-        make_identity(nc, ident[:])
+        ident0 = new_tile([P, P], F32, "ident0")
+        make_identity(nc, ident0[:])
 
         w2c = new_tile([P, 2 * H], U8, "w2c")
         w2s = new_tile([P, H], U8, "w2s")
@@ -138,7 +139,7 @@ def tile_list_woven_probe_lighting_kernel(
                 nc.scalar.activation(h2[t][:, cols], h2[t][:, cols], ACT.Copy, scale=tint_sb[:, t : t + 1])
 
         def scatter(t, places, h, wg):
-            nc.vector.tensor_tensor(page[t][:].indirect(places[:]), h[t][:], wg[t], MULT)
+            nc.vector.tensor_tensor(page[t][:].indirect(places[:]), h[t][:], wg[t][:], MULT)
 
         glossy(0)
         g1w = new_tile([P, 2, S], U32, "g1w")
@@ -160,8 +161,7 @@ def tile_list_woven_probe_lighting_kernel(
             glossy(t)
         warm = new_tile([P, 1], F32, "warm")
         nc.scalar.activation(warm[:], h2[PACK - 1][:, S - 1 : S], ACT.Sigmoid)
-        for t in range(1, PACK - 1):
-            scatter(t, o4, h2, wg2_sb)
+        scatter(1, o4, h2, wg2_sb)
 
         for t in range(PACK):
             for b in range(2):
@@ -179,6 +179,8 @@ def tile_list_woven_probe_lighting_kernel(
                     )
                 nc.scalar.activation(h1[t][:, cols], acc[:], ACT.Relu)
 
+        ident = new_tile([P, P], F32, "ident", "g1s")
+        nc.scalar.copy(ident[:], ident0[:])
         wab = new_tile([P, N, PACK], BF16, "wab")
         nc.scalar.copy(wab[:], waraw[:].rearrange("p j n -> p n j"))
         wac = new_tile([P, N], U32, "wac")
@@ -187,20 +189,23 @@ def tile_list_woven_probe_lighting_kernel(
 
         hist_rows = hist.rearrange("(p t) m -> t p m", t=PACK)
         hist_sb = []
-        for t, tag in enumerate(("g1w", "tab2w", "tabw0")):
+        for t, tag in enumerate(("hist0", "tab2w", "tabw0", "tabw1")):
             rows = new_tile([P, T2], F32, f"hist{t}", tag)
             nc.sync.dma_start(rows[:], hist_rows[t])
             hist_sb.append(rows)
 
         for t in range(PACK - 1):
             scatter(t, o3, h1, wg1_sb)
-        wg2_sb = wg2_sb + load_wg(wg2, 3, 4, "wg2c", "wg1a")
-        scatter(PACK - 1, o4, h2, wg2_sb)
+        for t in (2, 3):
+            wg2_sb.append(load_wg(wg2, t, f"wg2_{t}", f"wg1_{t - 2}"))
+            scatter(t, o4, h2, wg2_sb)
+        wg1_sb.append(load_wg(wg1, 3, "wg1_3", "wg1_0"))
         scatter(PACK - 1, o3, h1, wg1_sb)
 
         chunks = T2 // BANK
         blocks = BANK // P
-        zt = [new_tile([P, blocks, P, 2], BF16, f"zt{c}") for c in range(chunks)]
+        zt_all = shared.tile([P, chunks, blocks, P, 2], BF16, name="zt_all", align_bytes=AL, offset=2048)
+        zt = [zt_all[:, c, :, :, :] for c in range(chunks)]
         pairs = [new_tile([P, 2, BANK], F32, f"pairs{c}") for c in range(chunks)]
 
         def add_turned(t, c):
@@ -213,7 +218,7 @@ def tile_list_woven_probe_lighting_kernel(
 
         def turn_back(u, c):
             bank = ps.tile([P, blocks, P], F32, name="bank", tag="tr")
-            words = zt[c][:].rearrange("m b p e -> m (b p e)").bitcast(F32)
+            words = zt[c].rearrange("m b p e -> m (b p e)").bitcast(F32)
             for blk in range(blocks):
                 nc.tensor.transpose(bank[:, blk, :], words[:, P * blk : P * (blk + 1)], ident[:])
             nc.scalar.copy(pairs[c][:, u, :], bank[:].rearrange("p b m -> p (b m)"))
@@ -225,16 +230,13 @@ def tile_list_woven_probe_lighting_kernel(
                 add_turned(t, c)
             for c in range(chunks):
                 turn_back(t - 1, c)
-        rows = new_tile([P, T2], F32, "hist3", "tabw0")
-        nc.sync.dma_start(rows[:], hist_rows[PACK - 1])
-        hist_sb.append(rows)
 
         free_tags = h2_tags + [f"h1_{t}" for t in range(PACK)]
         for c in range(chunks):
             cols = slice(BANK * c, BANK * (c + 1))
             halves = pairs[c][:, 1, :].bitcast(BF16).rearrange("p (m e) -> p m e", e=2)
             nc.vector.tensor_tensor(halves[:, :, 1], page[PACK - 1][:, cols], hist_sb[PACK - 1][:, cols], ADD)
-            zb = new_tile([P, BANK, 2], F32, "zb", bufs=3)
+            zb = shared.tile([P, BANK, 2], F32, name=f"zb{c}", align_bytes=AL, offset=4096 * (c % 3))
             nc.scalar.copy(zb[:], pairs[c][:].rearrange("p u m -> p m u"))
             zc = new_tile([P, BANK], U32, "zc", bufs=3)
             zs = new_tile([P, BANK], U8, "zs", bufs=3)

@@ -69,10 +69,10 @@ def tile_list_woven_probe_lighting_kernel(
             return dst
 
         o2 = load_list(offs2, "o2")
-        tab2s = load_scales(tab2_scales, "tab2s", nc.gpsimd, nc.sync)
-        o1 = load_list(offs, "o1")
         w2raw = new_tile([P, 2 * H], U8, "w2raw")
         nc.sync.dma_start(w2raw[:].bitcast(I32), w2_words[0].bitcast(I32))
+        tab2s = load_scales(tab2_scales, "tab2s", nc.gpsimd, nc.sync)
+        o1 = load_list(offs, "o1")
         tab2w = load_words(tab2_words[0], "tab2w")
         tabs = load_scales(tab_scales, "tabs", nc.gpsimd, nc.sync)
         w2sraw = load_scales(w2_scales, "w2sraw", nc.gpsimd, nc.sync)
@@ -96,12 +96,16 @@ def tile_list_woven_probe_lighting_kernel(
         ident0 = new_tile([P, P], F32, "ident0")
         make_identity(nc, ident0[:])
 
-        w2c = new_tile([P, 2 * H], U8, "w2c")
+        def w2_codes(u, tag):
+            dst = new_tile([P, H], U8, f"w2c{u}", tag)
+            nc.vector.tensor_copy(
+                dst[:].bitcast(U16).rearrange("p (t m) -> p t m", t=2),
+                w2raw[:].bitcast(U16).rearrange("p (m t) -> p t m", t=PACK)[:, 2 * u : 2 * u + 2, :],
+            )
+            return dst
+
+        w2c = [w2_codes(0, "w2c0")]
         w2s = new_tile([P, H], U8, "w2s")
-        nc.vector.tensor_copy(
-            w2c[:].bitcast(U16).rearrange("p (t m) -> p t m", t=PACK),
-            w2raw[:].bitcast(U16).rearrange("p (m t) -> p t m", t=PACK),
-        )
         nc.vector.tensor_copy(
             w2s[:].rearrange("p (t m) -> p t m", t=PACK),
             w2sraw[:].rearrange("p (m t) -> p t m", t=PACK),
@@ -127,7 +131,7 @@ def tile_list_woven_probe_lighting_kernel(
                 acc = ps.tile([P, BANK], F32, name="acc", tag="mm")
                 nc.tensor.matmul_mx(
                     acc[:],
-                    lhsT=w2c[:, 2 * P * t : 2 * P * (t + 1)].bitcast(FP4X4),
+                    lhsT=w2c[t // 2][:, 2 * P * (t % 2) : 2 * P * (t % 2 + 1)].bitcast(FP4X4),
                     lhsT_scale=w2s[:, P * t : P * (t + 1)],
                     rhs=g2w[:, cols].bitcast(FP8X4),
                     rhs_scale=g2s[:, cols],
@@ -157,10 +161,7 @@ def tile_list_woven_probe_lighting_kernel(
         w1s = new_tile([P, PACK * 2 * P], U8, "w1s")
         nc.vector.quantize_mx(w1c[:].bitcast(FP8X4), w1s[:], w1b[:].rearrange("p t a m j -> p (t a m j)"))
 
-        for t in range(1, PACK):
-            glossy(t)
-        warm = new_tile([P, 1], F32, "warm")
-        nc.scalar.activation(warm[:], h2[PACK - 1][:, S - 1 : S], ACT.Sigmoid)
+        glossy(1)
         scatter(1, o4, h2, wg2_sb)
 
         for t in range(PACK):
@@ -186,6 +187,12 @@ def tile_list_woven_probe_lighting_kernel(
         wac = new_tile([P, N], U32, "wac")
         was = new_tile([P, N], U8, "was")
         nc.vector.quantize_mx(wac[:].bitcast(FP8X4), was[:], wab[:].rearrange("p n j -> p (n j)"))
+
+        w2c.append(w2_codes(1, "wg2_1"))
+        for t in (2, 3):
+            glossy(t)
+        warm = new_tile([P, 1], F32, "warm")
+        nc.scalar.activation(warm[:], h2[PACK - 1][:, S - 1 : S], ACT.Sigmoid)
 
         hist_rows = hist.rearrange("(p t) m -> t p m", t=PACK)
         hist_sb = []
@@ -253,5 +260,8 @@ def tile_list_woven_probe_lighting_kernel(
                 gate = new_tile([P, BANK], F32, "gate", bufs=3)
                 nc.scalar.activation(gate[:], vis[:], ACT.Sigmoid)
                 res = new_tile([P, BANK], F32, "res", free_tags[2 * c + n])
-                nc.vector.tensor_tensor(res[:], light[:], gate[:], MULT)
-                nc.sync.dma_start(out[rows, cols], res[:])
+                width = BANK // 2 if (c, n) == (chunks - 1, N // P - 1) else BANK
+                for lo in range(0, BANK, width):
+                    part = slice(lo, lo + width)
+                    nc.vector.tensor_tensor(res[:, part], light[:, part], gate[:, part], MULT)
+                    nc.sync.dma_start(out[rows, BANK * c + lo : BANK * c + lo + width], res[:, part])

@@ -68,60 +68,89 @@ def tile_list_woven_probe_lighting_kernel(
                 nc.sync.dma_start(dst[QUAD * g : QUAD * (g + 1), :], rows[t])
             return dst
 
+        def load_wg_pairs(src, name):
+            dst = new_tile([P, S], F32, name)
+            rows = src.rearrange("(q t) j -> q t j", t=PACK)[:, 0:2, :]
+            for g in range(2):
+                nc.sync.dma_start(dst[64 * g : 64 * (g + 1), :], rows)
+            return dst
+
         o2 = load_list(offs2, "o2")
+        tab2s = new_tile([P, T], U8, "tab2s")
+        for q in range(4):
+            nc.sync.dma_start(
+                tab2s[QUAD * q : QUAD * (q + 1), :].bitcast(I32),
+                tab2_scales[0, 4 * q : 4 * q + 4, :].bitcast(I32).partition_broadcast(QUAD // 4),
+            )
+        tab2w = load_words(tab2_words[0], "tab2w")
+        o1 = load_list(offs, "o1")
+        tabw = [load_words(tab_words[0], "tabw0")]
+        w2sraw = load_scales(w2_scales, "w2sraw", nc.gpsimd, nc.sync)
         w2raw = new_tile([P, 2 * H], U8, "w2raw")
         nc.sync.dma_start(w2raw[:].bitcast(I32), w2_words[0].bitcast(I32))
-        tab2s = load_scales(tab2_scales, "tab2s", nc.gpsimd, nc.sync)
-        o1 = load_list(offs, "o1")
-        tab2w = load_words(tab2_words[0], "tab2w")
+        tabw.append(load_words(tab_words[1], "tabw1"))
         tabs = load_scales(tab_scales, "tabs", nc.gpsimd, nc.sync)
-        w2sraw = load_scales(w2_scales, "w2sraw", nc.gpsimd, nc.sync)
-        tabw = [load_words(tab_words[a], f"tabw{a}") for a in range(2)]
-        tint_sb = new_tile([P, PACK], F32, "tint_sb")
-        nc.sync.dma_start(tint_sb[:], tint.rearrange("(p t) -> p t", t=PACK))
+        tint_lo = []
+        for h in range(2):
+            col = new_tile([P, 1], F32, f"tint_lo{h}")
+            nc.sync.dma_start(col[:], tint[256 * h : 256 * (h + 1)].rearrange("(q t) -> q t", t=PACK)[:, 0:2])
+            tint_lo.append(col)
         o4 = load_list(offs4, "o4")
-        wg2_sb = [load_wg(wg2, 0, "wg2_0")]
+        wg2_pairs = load_wg_pairs(wg2, "wg2_pairs")
         w1raw = []
         for a in range(2):
             raw = new_tile([P, PACK, H], F32, f"w1raw{a}")
             nc.sync.dma_start(raw[:], w1[512 * a : 512 * (a + 1), :].rearrange("(p j) c -> p j c", j=PACK))
             w1raw.append(raw)
-        wg2_sb.append(load_wg(wg2, 1, "wg2_1"))
+        tint_hi = new_tile([P, PACK], F32, "tint_hi")
+        nc.sync.dma_start(tint_hi[:], tint.rearrange("(p t) -> p t", t=PACK))
+        tints = [tint_lo[0][:], tint_lo[1][:], tint_hi[:, 2:3], tint_hi[:, 3:4]]
+        wg2_sb = [wg2_pairs, wg2_pairs, load_wg(wg2, 2, "wg2_2")]
         o3 = load_list(offs3, "o3")
-        wg1_sb = [load_wg(wg1, t, f"wg1_{t}") for t in range(PACK - 1)]
+        wg1_pairs = load_wg_pairs(wg1, "wg1_pairs")
         waraw = new_tile([P, PACK, N], F32, "waraw")
         nc.sync.dma_start(waraw[:], wa.rearrange("(p j) c -> p j c", j=PACK))
+        hist_sb = []
+        for t, tag in enumerate(("hist0", "tab2w", "tabw0", "tabw1")):
+            rows = new_tile([P, T2], F32, f"hist{t}", tag)
+            if t < 2:
+                src = hist[256 * t : 256 * (t + 1), :].rearrange("(q t) m -> q t m", t=PACK)[:, 0:2, :]
+            else:
+                src = hist.rearrange("(p t) m -> t p m", t=PACK)[t]
+            nc.sync.dma_start(rows[:], src)
+            hist_sb.append(rows)
+        wg1_sb = [wg1_pairs, wg1_pairs, load_wg(wg1, 2, "wg1_2"), load_wg(wg1, 3, "wg1_3")]
         wbw = load_words(wb_words[0], "wbw")
         wbs = load_scales(wb_scales, "wbs", nc.gpsimd, nc.sync)
         ident0 = new_tile([P, P], F32, "ident0")
         make_identity(nc, ident0[:])
 
-        def w2_codes(u, tag):
-            dst = new_tile([P, H], U8, f"w2c{u}", tag)
-            nc.vector.tensor_copy(
-                dst[:].bitcast(U16).rearrange("p (t m) -> p t m", t=2),
-                w2raw[:].bitcast(U16).rearrange("p (m t) -> p t m", t=PACK)[:, 2 * u : 2 * u + 2, :],
-            )
-            return dst
-
-        w2c = [w2_codes(0, "w2c0")]
-        w2s = new_tile([P, H], U8, "w2s")
-        nc.vector.tensor_copy(
-            w2s[:].rearrange("p (t m) -> p t m", t=PACK),
-            w2sraw[:].rearrange("p (m t) -> p t m", t=PACK),
-        )
-
         g2s = new_tile([P, S], U8, "g2s")
         nc.vector.tensor_copy(g2s[:], tab2s[:].indirect(o2[:]))
         g2w = new_tile([P, S], U32, "g2w")
-        for b in range(2):
-            nc.vector.tensor_copy(g2w[:, BANK * b : BANK * (b + 1)], tab2w[:].indirect(o2[:, 32 * b : 32 * (b + 1)]))
+        nc.vector.tensor_copy(g2w[:], tab2w[:].indirect(o2[:]))
+        g1w = new_tile([P, 2, S], U32, "g1w")
+        nc.vector.tensor_copy(g1w[:, 0, :], tabw[0][:].indirect(o1[:]))
+
+        w2c = new_tile([P, 2 * H], U8, "w2c")
+        w2s = new_tile([P, H], U8, "w2s")
+        nc.vector.tensor_copy(w2c[:, 0:H].bitcast(U32), w2raw[:].bitcast(U32).rearrange("p (q u) -> p q u", u=2)[:, :, 0])
+        nc.vector.tensor_copy(w2s[:, 0 : H // 2].bitcast(U16), w2sraw[:].bitcast(U16).rearrange("p (q u) -> p q u", u=2)[:, :, 0])
+        nc.vector.tensor_copy(
+            w2c[:, H : 2 * H].bitcast(U16).rearrange("p (t m) -> p t m", t=2),
+            w2raw[:].bitcast(U16).rearrange("p (m t) -> p t m", t=PACK)[:, 2:4, :],
+        )
+        nc.vector.tensor_copy(
+            w2s[:, H // 2 : H].rearrange("p (t m) -> p t m", t=2),
+            w2sraw[:].rearrange("p (m t) -> p t m", t=PACK)[:, 2:4, :],
+        )
+        nc.vector.tensor_copy(g1w[:, 1, :], tabw[1][:].indirect(o1[:]))
         g1s = new_tile([P, S], U8, "g1s")
         nc.vector.tensor_copy(g1s[:], tabs[:].indirect(o1[:]))
 
         page = [new_tile([P, T2], F32, f"page{t}") for t in range(PACK)]
         h1 = [new_tile([P, S], F32, f"h1_{t}") for t in range(PACK)]
-        h2_tags = ["h2_0", "w1raw1", "w1raw0", "w1b"]
+        h2_tags = ["h2_0", "h2_1", "w1raw1", "w1b"]
         h2 = []
 
         def glossy(t):
@@ -131,7 +160,7 @@ def tile_list_woven_probe_lighting_kernel(
                 acc = ps.tile([P, BANK], F32, name="acc", tag="mm")
                 nc.tensor.matmul_mx(
                     acc[:],
-                    lhsT=w2c[t // 2][:, 2 * P * (t % 2) : 2 * P * (t % 2 + 1)].bitcast(FP4X4),
+                    lhsT=w2c[:, 2 * P * t : 2 * P * (t + 1)].bitcast(FP4X4),
                     lhsT_scale=w2s[:, P * t : P * (t + 1)],
                     rhs=g2w[:, cols].bitcast(FP8X4),
                     rhs_scale=g2s[:, cols],
@@ -140,36 +169,36 @@ def tile_list_woven_probe_lighting_kernel(
                 nc.scalar.activation(h2[t][:, cols], acc[:], ACT.Exp)
             for b in range(2):
                 cols = slice(BANK * b, BANK * (b + 1))
-                nc.scalar.activation(h2[t][:, cols], h2[t][:, cols], ACT.Copy, scale=tint_sb[:, t : t + 1])
+                nc.scalar.activation(h2[t][:, cols], h2[t][:, cols], ACT.Copy, scale=tints[t])
 
         def scatter(t, places, h, wg):
             nc.vector.tensor_tensor(page[t][:].indirect(places[:]), h[t][:], wg[t][:], MULT)
 
-        glossy(0)
-        g1w = new_tile([P, 2, S], U32, "g1w")
-        for a in range(2):
-            nc.vector.tensor_copy(g1w[:, a, :], tabw[a][:].indirect(o1[:]))
-        scatter(0, o4, h2, wg2_sb)
+        for t in range(2):
+            glossy(t)
+            scatter(t, o4, h2, wg2_sb)
 
-        w1b = new_tile([P, PACK, 2, P, PACK], BF16, "w1b")
+        w1b = new_tile([P, 2, PACK, P, PACK], BF16, "w1b")
         for a in range(2):
+            by_four = w1raw[a][:].rearrange("p j (m t) -> p m t j", t=PACK)
             nc.scalar.copy(
-                w1b[:, :, a, :, :].rearrange("p t m j -> p m t j"),
-                w1raw[a][:].rearrange("p j (m t) -> p m t j", t=PACK),
+                w1b[:, a, 0:2, :, :].rearrange("p h (q e) j -> p (h q) e j", e=2),
+                by_four[:, :, 0:2, :],
             )
+            nc.scalar.copy(w1b[:, a, 2:4, :, :].rearrange("p t m j -> p m t j"), by_four[:, :, 2:4, :])
         w1c = new_tile([P, PACK * 2 * P], U32, "w1c")
         w1s = new_tile([P, PACK * 2 * P], U8, "w1s")
-        nc.vector.quantize_mx(w1c[:].bitcast(FP8X4), w1s[:], w1b[:].rearrange("p t a m j -> p (t a m j)"))
+        nc.vector.quantize_mx(w1c[:].bitcast(FP8X4), w1s[:], w1b[:].rearrange("p a t m j -> p (a t m j)"))
 
-        glossy(1)
-        scatter(1, o4, h2, wg2_sb)
+        glossy(2)
+        scatter(2, o4, h2, wg2_sb)
 
         for t in range(PACK):
             for b in range(2):
                 cols = slice(BANK * b, BANK * (b + 1))
                 acc = ps.tile([P, BANK], F32, name="acc", tag="mm")
                 for a in range(2):
-                    wcols = slice(P * (2 * t + a), P * (2 * t + a + 1))
+                    wcols = slice(P * (PACK * a + t), P * (PACK * a + t + 1))
                     nc.tensor.matmul_mx(
                         acc[:],
                         lhsT=w1c[:, wcols].bitcast(FP8X4),
@@ -188,25 +217,14 @@ def tile_list_woven_probe_lighting_kernel(
         was = new_tile([P, N], U8, "was")
         nc.vector.quantize_mx(wac[:].bitcast(FP8X4), was[:], wab[:].rearrange("p n j -> p (n j)"))
 
-        w2c.append(w2_codes(1, "wg2_1"))
-        for t in (2, 3):
-            glossy(t)
+        glossy(3)
         warm = new_tile([P, 1], F32, "warm")
         nc.scalar.activation(warm[:], h2[PACK - 1][:, S - 1 : S], ACT.Sigmoid)
 
-        hist_rows = hist.rearrange("(p t) m -> t p m", t=PACK)
-        hist_sb = []
-        for t, tag in enumerate(("hist0", "tab2w", "tabw0", "tabw1")):
-            rows = new_tile([P, T2], F32, f"hist{t}", tag)
-            nc.sync.dma_start(rows[:], hist_rows[t])
-            hist_sb.append(rows)
-
         for t in range(PACK - 1):
             scatter(t, o3, h1, wg1_sb)
-        for t in (2, 3):
-            wg2_sb.append(load_wg(wg2, t, f"wg2_{t}", f"wg1_{t - 2}"))
-            scatter(t, o4, h2, wg2_sb)
-        wg1_sb.append(load_wg(wg1, 3, "wg1_3", "wg1_0"))
+        wg2_sb.append(load_wg(wg2, 3, "wg2_3", "wg1_pairs"))
+        scatter(PACK - 1, o4, h2, wg2_sb)
         scatter(PACK - 1, o3, h1, wg1_sb)
 
         chunks = T2 // BANK
@@ -221,7 +239,10 @@ def tile_list_woven_probe_lighting_kernel(
                 cols = slice(BANK * c + P * blk, BANK * c + P * (blk + 1))
                 nc.tensor.matmul(bank[:, blk, :], lhsT=hist_sb[t][:, cols], rhs=ident[:], is_transpose=True, start=True, stop=False)
                 nc.tensor.matmul(bank[:, blk, :], lhsT=page[t][:, cols], rhs=ident[:], is_transpose=True, start=False, stop=True)
-            nc.scalar.copy(zt[c][:, :, :, t % 2], bank[:])
+            if t < 2:
+                nc.scalar.copy(zt[c].rearrange("m b p e -> m b (p e)")[:, :, P * t : P * (t + 1)], bank[:])
+            else:
+                nc.scalar.copy(zt[c][:, :, :, 0], bank[:])
 
         def turn_back(u, c):
             bank = ps.tile([P, blocks, P], F32, name="bank", tag="tr")

@@ -134,13 +134,16 @@ def tile_list_woven_probe_lighting_kernel(
 
         w2c = new_tile([P, 2 * H], U8, "w2c")
         w2s = new_tile([P, H], U8, "w2s")
-        nc.vector.tensor_copy(w2c[:, 0:H].bitcast(U32), w2raw[:].bitcast(U32).rearrange("p (q u) -> p q u", u=2)[:, :, 0])
-        nc.vector.tensor_copy(w2s[:, 0 : H // 2].bitcast(U16), w2sraw[:].bitcast(U16).rearrange("p (q u) -> p q u", u=2)[:, :, 0])
-        nc.vector.tensor_copy(
-            w2c[:, H : 2 * H].bitcast(U16).rearrange("p (t m) -> p t m", t=2),
-            w2raw[:].bitcast(U16).rearrange("p (m t) -> p t m", t=PACK)[:, 2:4, :],
+        nc.gpsimd.tensor_copy(w2c[:, 0:H].bitcast(U32), w2raw[:].bitcast(U32).rearrange("p (q u) -> p q u", u=2)[:, :, 0])
+        nc.gpsimd.tensor_copy(
+            w2s[:, 0 : H // 2].rearrange("p (q e) -> p q e", e=2),
+            w2sraw[:].rearrange("p (q t) -> p q t", t=PACK)[:, :, 0:2],
         )
-        nc.vector.tensor_copy(
+        nc.gpsimd.tensor_copy(
+            w2c[:, H : 2 * H].rearrange("p (t m b) -> p t m b", t=2, b=2),
+            w2raw[:].rearrange("p (m t b) -> p t m b", t=PACK, b=2)[:, 2:4, :, :],
+        )
+        nc.gpsimd.tensor_copy(
             w2s[:, H // 2 : H].rearrange("p (t m) -> p t m", t=2),
             w2sraw[:].rearrange("p (m t) -> p t m", t=PACK)[:, 2:4, :],
         )
@@ -239,10 +242,7 @@ def tile_list_woven_probe_lighting_kernel(
                 cols = slice(BANK * c + P * blk, BANK * c + P * (blk + 1))
                 nc.tensor.matmul(bank[:, blk, :], lhsT=hist_sb[t][:, cols], rhs=ident[:], is_transpose=True, start=True, stop=False)
                 nc.tensor.matmul(bank[:, blk, :], lhsT=page[t][:, cols], rhs=ident[:], is_transpose=True, start=False, stop=True)
-            if t < 2:
-                nc.scalar.copy(zt[c].rearrange("m b p e -> m b (p e)")[:, :, P * t : P * (t + 1)], bank[:])
-            else:
-                nc.scalar.copy(zt[c][:, :, :, 0], bank[:])
+            nc.scalar.copy(zt[c].rearrange("m b p e -> m b (p e)")[:, :, P * t : P * (t + 1)], bank[:])
 
         def turn_back(u, c):
             bank = ps.tile([P, blocks, P], F32, name="bank", tag="tr")
@@ -251,24 +251,42 @@ def tile_list_woven_probe_lighting_kernel(
                 nc.tensor.transpose(bank[:, blk, :], words[:, P * blk : P * (blk + 1)], ident[:])
             nc.scalar.copy(pairs[c][:, u, :], bank[:].rearrange("p b m -> p (b m)"))
 
-        for c in range(chunks):
-            add_turned(0, c)
-        for t in (1, 2):
+        for t in range(2):
             for c in range(chunks):
                 add_turned(t, c)
-            for c in range(chunks):
-                turn_back(t - 1, c)
+        for c in range(chunks):
+            turn_back(0, c)
+        held = []
+        for c in range(chunks):
+            bank = ps.tile([P, blocks, P], F32, name="held", tag="mm")
+            for blk in range(blocks):
+                cols = slice(BANK * c + P * blk, BANK * c + P * (blk + 1))
+                nc.tensor.matmul(bank[:, blk, :], lhsT=hist_sb[2][:, cols], rhs=ident[:], is_transpose=True, start=(blk == 0), stop=False)
+            held.append(bank)
+        for c in range(chunks):
+            for blk in range(blocks):
+                cols = slice(BANK * c + P * blk, BANK * c + P * (blk + 1))
+                nc.tensor.matmul(held[c][:, blk, :], lhsT=page[2][:, cols], rhs=ident[:], is_transpose=True, start=False, stop=(blk == blocks - 1))
+            nc.scalar.copy(zt[c][:, :, :, 0], held[c][:])
+        for c in range(chunks):
+            turn_back(1, c)
 
+        z = []
         free_tags = h2_tags + [f"h1_{t}" for t in range(PACK)]
         for c in range(chunks):
             cols = slice(BANK * c, BANK * (c + 1))
             halves = pairs[c][:, 1, :].bitcast(BF16).rearrange("p (m e) -> p m e", e=2)
             nc.vector.tensor_tensor(halves[:, :, 1], page[PACK - 1][:, cols], hist_sb[PACK - 1][:, cols], ADD)
-            zb = shared.tile([P, BANK, 2], F32, name=f"zb{c}", align_bytes=AL, offset=4096 * (c % 3))
-            nc.scalar.copy(zb[:], pairs[c][:].rearrange("p u m -> p m u"))
-            zc = new_tile([P, BANK], U32, "zc", bufs=3)
-            zs = new_tile([P, BANK], U8, "zs", bufs=3)
+            zb = shared.tile([P, BANK, 2], F32, name=f"zb{c}", align_bytes=AL, offset=4096 * c)
+            if c < chunks - 1:
+                nc.scalar.copy(zb[:], pairs[c][:].rearrange("p u m -> p m u"))
+            else:
+                nc.vector.tensor_copy(zb[:], pairs[c][:].rearrange("p u m -> p m u"))
+            zc = new_tile([P, BANK], U32, f"zc{c}")
+            zs = new_tile([P, BANK], U8, f"zs{c}")
             nc.vector.quantize_mx(zc[:].bitcast(FP8X4), zs[:], zb[:].rearrange("p m u -> p (m u)").bitcast(BF16))
+            z.append((zc, zs))
+        for c, (zc, zs) in enumerate(z):
             for n in range(N // P):
                 rows = slice(P * n, P * (n + 1))
                 vis = ps.tile([P, BANK], F32, name="vis", tag="mm")

@@ -251,6 +251,15 @@ def tile_list_woven_probe_lighting_kernel(
                 nc.tensor.transpose(bank[:, blk, :], words[:, P * blk : P * (blk + 1)], ident[:])
             nc.scalar.copy(pairs[c][:, u, :], bank[:].rearrange("p b m -> p (b m)"))
 
+        on_vector = (0, 1, 3)
+        hist_t = new_tile([P, len(on_vector), BANK], F32, "hist_t", "w1raw0")
+        for i, c in enumerate(on_vector):
+            bank = ps.tile([P, blocks, P], F32, name="bank", tag="tr")
+            for blk in range(blocks):
+                cols = slice(BANK * c + P * blk, BANK * c + P * (blk + 1))
+                nc.tensor.transpose(bank[:, blk, :], hist_sb[PACK - 1][:, cols], ident[:])
+            nc.scalar.copy(hist_t[:, i, :], bank[:].rearrange("m b p -> m (b p)"))
+
         for t in range(2):
             for c in range(chunks):
                 add_turned(t, c)
@@ -268,39 +277,63 @@ def tile_list_woven_probe_lighting_kernel(
                 cols = slice(BANK * c + P * blk, BANK * c + P * (blk + 1))
                 nc.tensor.matmul(held[c][:, blk, :], lhsT=page[2][:, cols], rhs=ident[:], is_transpose=True, start=False, stop=(blk == blocks - 1))
             nc.scalar.copy(zt[c][:, :, :, 0], held[c][:])
+        hist_ps = {}
+        for i, c in enumerate(on_vector):
+            bank = ps.tile([P, blocks, P], F32, name="hist_ps", tag="mm")
+            for blk in range(blocks):
+                nc.tensor.transpose(bank[:, blk, :], hist_t[:, i, P * blk : P * (blk + 1)], ident[:])
+            hist_ps[c] = bank
         for c in range(chunks):
             turn_back(1, c)
 
-        z = []
         free_tags = h2_tags + [f"h1_{t}" for t in range(PACK)]
-        for c in range(chunks):
-            cols = slice(BANK * c, BANK * (c + 1))
+        zb = [shared.tile([P, BANK, 2], F32, name=f"zb{c}", align_bytes=AL, offset=4096 * c) for c in range(chunks)]
+        woven = [pairs[c][:].rearrange("p u m -> p m u") for c in range(chunks)]
+        z = [(new_tile([P, BANK], U32, f"zc{c}"), new_tile([P, BANK], U8, f"zs{c}")) for c in range(chunks)]
+        last = page[PACK - 1]
+
+        def hist_bank(c):
+            return hist_ps[c][:].rearrange("p b m -> p (b m)")
+
+        def fourth(c):
+            return zb[c][:].rearrange("p m u -> p (m u)").bitcast(BF16).rearrange("p (m j) -> p m j", j=PACK)[:, :, PACK - 1]
+
+        def quantise(c):
+            nc.vector.quantize_mx(z[c][0][:].bitcast(FP8X4), z[c][1][:], zb[c][:].rearrange("p m u -> p (m u)").bitcast(BF16))
+
+        for c in (2, 3):
+            nc.scalar.copy(zb[c][:], woven[c])
+        for c in (0, 1):
             halves = pairs[c][:, 1, :].bitcast(BF16).rearrange("p (m e) -> p m e", e=2)
-            nc.vector.tensor_tensor(halves[:, :, 1], page[PACK - 1][:, cols], hist_sb[PACK - 1][:, cols], ADD)
-            zb = shared.tile([P, BANK, 2], F32, name=f"zb{c}", align_bytes=AL, offset=4096 * c)
-            if c < chunks - 1:
-                nc.scalar.copy(zb[:], pairs[c][:].rearrange("p u m -> p m u"))
-            else:
-                nc.vector.tensor_copy(zb[:], pairs[c][:].rearrange("p u m -> p m u"))
-            zc = new_tile([P, BANK], U32, f"zc{c}")
-            zs = new_tile([P, BANK], U8, f"zs{c}")
-            nc.vector.quantize_mx(zc[:].bitcast(FP8X4), zs[:], zb[:].rearrange("p m u -> p (m u)").bitcast(BF16))
-            z.append((zc, zs))
-        for c, (zc, zs) in enumerate(z):
-            for n in range(N // P):
+            nc.vector.tensor_tensor(halves[:, :, 1], hist_bank(c), last[:, BANK * c : BANK * (c + 1)], ADD)
+            nc.scalar.copy(zb[c][:], woven[c])
+        cut = 192
+        nc.vector.tensor_tensor(fourth(3)[:, 0:cut], hist_bank(3)[:, 0:cut], last[:, BANK * 3 : BANK * 3 + cut], ADD)
+        nc.gpsimd.tensor_tensor(fourth(2), last[:, BANK * 2 : BANK * 3], hist_sb[PACK - 1][:, BANK * 2 : BANK * 3], ADD)
+        nc.gpsimd.tensor_tensor(fourth(3)[:, cut:], last[:, BANK * 3 + cut :], hist_sb[PACK - 1][:, BANK * 3 + cut :], ADD)
+        order = (2, 0, 3, 1)
+        for c in order:
+            quantise(c)
+        for i, c in enumerate(order):
+            zc, zs = z[c]
+
+            def product(name, tag, wc, ws, n):
+                acc = ps.tile([P, BANK], F32, name=name, tag=tag)
                 rows = slice(P * n, P * (n + 1))
-                vis = ps.tile([P, BANK], F32, name="vis", tag="mm")
-                light = ps.tile([P, BANK], F32, name="light", tag="tr")
-                for acc, wc, ws in ((vis, wbw, wbs), (light, wac, was)):
-                    nc.tensor.matmul_mx(
-                        acc[:], lhsT=wc[:, rows].bitcast(FP8X4), lhsT_scale=ws[:, rows],
-                        rhs=zc[:].bitcast(FP8X4), rhs_scale=zs[:], start=True, stop=True,
-                    )
+                nc.tensor.matmul_mx(
+                    acc[:], lhsT=wc[:, rows].bitcast(FP8X4), lhsT_scale=ws[:, rows],
+                    rhs=zc[:].bitcast(FP8X4), rhs_scale=zs[:], start=True, stop=True,
+                )
+                return acc
+
+            vis = [product("vis", "mm", wbw, wbs, n) for n in range(N // P)]
+            light = [product("light", "tr", wac, was, n) for n in range(N // P)]
+            for n in range(N // P):
                 gate = new_tile([P, BANK], F32, "gate", bufs=3)
-                nc.scalar.activation(gate[:], vis[:], ACT.Sigmoid)
-                res = new_tile([P, BANK], F32, "res", free_tags[2 * c + n])
-                width = BANK // 2 if (c, n) == (chunks - 1, N // P - 1) else BANK
+                nc.scalar.activation(gate[:], vis[n][:], ACT.Sigmoid)
+                res = new_tile([P, BANK], F32, "res", free_tags[2 * i + n])
+                width = BANK // 2 if (i, n) == (chunks - 1, N // P - 1) else BANK
                 for lo in range(0, BANK, width):
                     part = slice(lo, lo + width)
-                    nc.vector.tensor_tensor(res[:, part], light[:, part], gate[:, part], MULT)
-                    nc.sync.dma_start(out[rows, BANK * c + lo : BANK * c + lo + width], res[:, part])
+                    nc.vector.tensor_tensor(res[:, part], light[n][:, part], gate[:, part], MULT)
+                    nc.sync.dma_start(out[P * n : P * (n + 1), BANK * c + lo : BANK * c + lo + width], res[:, part])

@@ -251,7 +251,7 @@ def tile_list_woven_probe_lighting_kernel(
                 nc.tensor.transpose(bank[:, blk, :], words[:, P * blk : P * (blk + 1)], ident[:])
             nc.scalar.copy(pairs[c][:, u, :], bank[:].rearrange("p b m -> p (b m)"))
 
-        on_vector = (0, 1, 3)
+        on_vector = (0, 1, 2)
         hist_t = new_tile([P, len(on_vector), BANK], F32, "hist_t", "w1raw0")
         for i, c in enumerate(on_vector):
             bank = ps.tile([P, blocks, P], F32, name="bank", tag="tr")
@@ -283,9 +283,6 @@ def tile_list_woven_probe_lighting_kernel(
             for blk in range(blocks):
                 nc.tensor.transpose(bank[:, blk, :], hist_t[:, i, P * blk : P * (blk + 1)], ident[:])
             hist_ps[c] = bank
-        for c in range(chunks):
-            turn_back(1, c)
-
         free_tags = h2_tags + [f"h1_{t}" for t in range(PACK)]
         zb = [shared.tile([P, BANK, 2], F32, name=f"zb{c}", align_bytes=AL, offset=4096 * c) for c in range(chunks)]
         woven = [pairs[c][:].rearrange("p u m -> p m u") for c in range(chunks)]
@@ -301,39 +298,56 @@ def tile_list_woven_probe_lighting_kernel(
         def quantise(c):
             nc.vector.quantize_mx(z[c][0][:].bitcast(FP8X4), z[c][1][:], zb[c][:].rearrange("p m u -> p (m u)").bitcast(BF16))
 
-        for c in (2, 3):
-            nc.scalar.copy(zb[c][:], woven[c])
-        for c in (0, 1):
-            halves = pairs[c][:, 1, :].bitcast(BF16).rearrange("p (m e) -> p m e", e=2)
-            nc.vector.tensor_tensor(halves[:, :, 1], hist_bank(c), last[:, BANK * c : BANK * (c + 1)], ADD)
-            nc.scalar.copy(zb[c][:], woven[c])
-        cut = 192
-        nc.vector.tensor_tensor(fourth(3)[:, 0:cut], hist_bank(3)[:, 0:cut], last[:, BANK * 3 : BANK * 3 + cut], ADD)
-        nc.gpsimd.tensor_tensor(fourth(2), last[:, BANK * 2 : BANK * 3], hist_sb[PACK - 1][:, BANK * 2 : BANK * 3], ADD)
-        nc.gpsimd.tensor_tensor(fourth(3)[:, cut:], last[:, BANK * 3 + cut :], hist_sb[PACK - 1][:, BANK * 3 + cut :], ADD)
-        order = (2, 0, 3, 1)
-        for c in order:
-            quantise(c)
-        for i, c in enumerate(order):
-            zc, zs = z[c]
 
-            def product(name, tag, wc, ws, n):
-                acc = ps.tile([P, BANK], F32, name=name, tag=tag)
-                rows = slice(P * n, P * (n + 1))
-                nc.tensor.matmul_mx(
-                    acc[:], lhsT=wc[:, rows].bitcast(FP8X4), lhsT_scale=ws[:, rows],
-                    rhs=zc[:].bitcast(FP8X4), rhs_scale=zs[:], start=True, stop=True,
-                )
-                return acc
+        def product(c, name, tag, wc, ws, n):
+            acc = ps.tile([P, BANK], F32, name=name, tag=tag)
+            rows = slice(P * n, P * (n + 1))
+            nc.tensor.matmul_mx(
+                acc[:], lhsT=wc[:, rows].bitcast(FP8X4), lhsT_scale=ws[:, rows],
+                rhs=z[c][0][:].bitcast(FP8X4), rhs_scale=z[c][1][:], start=True, stop=True,
+            )
+            return acc
 
-            vis = [product("vis", "mm", wbw, wbs, n) for n in range(N // P)]
-            light = [product("light", "tr", wac, was, n) for n in range(N // P)]
+        def read_out(c, final=False):
+            if final:
+                vis = [product(c, "vis", "mm", wbw, wbs, n) for n in range(N // P)]
+                light = [product(c, "light", "tr", wac, was, n) for n in range(N // P)]
+            else:
+                both = [(product(c, "vis", "mm", wbw, wbs, n), product(c, "light", "tr", wac, was, n)) for n in range(N // P)]
+                vis, light = zip(*both)
             for n in range(N // P):
                 gate = new_tile([P, BANK], F32, "gate", bufs=3)
                 nc.scalar.activation(gate[:], vis[n][:], ACT.Sigmoid)
-                res = new_tile([P, BANK], F32, "res", free_tags[2 * i + n])
-                width = BANK // 2 if (i, n) == (chunks - 1, N // P - 1) else BANK
+                res = new_tile([P, BANK], F32, "res", free_tags[2 * c + n])
+                width = BANK // 2 if final and n == N // P - 1 else BANK
                 for lo in range(0, BANK, width):
                     part = slice(lo, lo + width)
                     nc.vector.tensor_tensor(res[:, part], light[n][:, part], gate[:, part], MULT)
                     nc.sync.dma_start(out[P * n : P * (n + 1), BANK * c + lo : BANK * c + lo + width], res[:, part])
+
+        def add_to_pairs(c, width):
+            halves = pairs[c][:, 1, :].bitcast(BF16).rearrange("p (m e) -> p m e", e=2)
+            nc.vector.tensor_tensor(halves[:, 0:width, 1], hist_bank(c)[:, 0:width], last[:, BANK * c : BANK * c + width], ADD)
+
+        half = BANK // 2
+        turn_back(1, 3)
+        nc.scalar.copy(zb[3][:], woven[3])
+        for c in range(3):
+            turn_back(1, c)
+        nc.scalar.copy(zb[2][:, half:, :], woven[2][:, half:, :])
+
+        nc.gpsimd.tensor_tensor(fourth(3), last[:, BANK * 3 :], hist_sb[PACK - 1][:, BANK * 3 :], ADD)
+        add_to_pairs(0, BANK)
+        add_to_pairs(1, BANK)
+        add_to_pairs(2, half)
+        quantise(3)
+        nc.vector.tensor_tensor(fourth(2)[:, half:], hist_bank(2)[:, half:], last[:, BANK * 2 + half : BANK * 3], ADD)
+        for c in (0, 1):
+            nc.scalar.copy(zb[c][:], woven[c])
+            quantise(c)
+        read_out(3)
+        nc.scalar.copy(zb[2][:, 0:half, :], woven[2][:, 0:half, :])
+        quantise(2)
+        read_out(0)
+        read_out(1)
+        read_out(2, final=True)

@@ -108,8 +108,6 @@ def tile_list_woven_probe_lighting_kernel(
         wg2_sb = [wg2_pairs, wg2_pairs, load_wg(wg2, 2, "wg2_2")]
         o3 = load_list(offs3, "o3")
         wg1_pairs = load_wg_pairs(wg1, "wg1_pairs")
-        waraw = new_tile([P, PACK, N], F32, "waraw")
-        nc.sync.dma_start(waraw[:], wa.rearrange("(p j) c -> p j c", j=PACK))
         hist_sb = []
         for t, tag in enumerate(("hist0", "tab2w", "tabw0", "tabw1")):
             rows = new_tile([P, T2], F32, f"hist{t}", tag)
@@ -214,21 +212,28 @@ def tile_list_woven_probe_lighting_kernel(
 
         ident = new_tile([P, P], F32, "ident", "g1s")
         nc.scalar.copy(ident[:], ident0[:])
-        wab = new_tile([P, N, PACK], BF16, "wab")
-        nc.scalar.copy(wab[:], waraw[:].rearrange("p j n -> p n j"))
-        wac = new_tile([P, N], U32, "wac")
-        was = new_tile([P, N], U8, "was")
-        nc.vector.quantize_mx(wac[:].bitcast(FP8X4), was[:], wab[:].rearrange("p n j -> p (n j)"))
-
         glossy(3)
         warm = new_tile([P, 1], F32, "warm")
         nc.scalar.activation(warm[:], h2[PACK - 1][:, S - 1 : S], ACT.Sigmoid)
 
         for t in range(PACK - 1):
             scatter(t, o3, h1, wg1_sb)
-        wg2_sb.append(load_wg(wg2, 3, "wg2_3", "wg1_pairs"))
+        wg2_last = new_tile([P, S], F32, "wg2_3", "wg1_pairs")
+        wg2_rows = wg2.rearrange("(q t) j -> t q j", t=PACK)[PACK - 1]
+        for g in (0, 2, 1):
+            nc.sync.dma_start(wg2_last[QUAD * g : QUAD * (g + 1), :], wg2_rows)
+        waraw = new_tile([P, PACK, N], F32, "waraw", "h1_1")
+        nc.sync.dma_start(waraw[:], wa.rearrange("(p j) c -> p j c", j=PACK))
+        nc.sync.dma_start(wg2_last[QUAD * 3 :, :], wg2_rows)
+        wg2_sb.append(wg2_last)
         scatter(PACK - 1, o4, h2, wg2_sb)
         scatter(PACK - 1, o3, h1, wg1_sb)
+        wab = new_tile([P, N, PACK], BF16, "wab")
+        nc.scalar.copy(wab[:], waraw[:].rearrange("p j n -> p n j"))
+        wac = new_tile([P, N], U32, "wac")
+        was = new_tile([P, N], U8, "was")
+        nc.vector.quantize_mx(wac[:].bitcast(FP8X4), was[:], wab[:].rearrange("p n j -> p (n j)"))
+
 
         chunks = T2 // BANK
         blocks = BANK // P

@@ -345,13 +345,13 @@ def tile_list_woven_probe_lighting_kernel(
         add_to_pairs(0, BANK)
         add_to_pairs(1, BANK)
         add_to_pairs(2, half)
-        quantise(3)
         nc.vector.tensor_tensor(fourth(2)[:, half:], hist_bank(2)[:, half:], last[:, BANK * 2 + half : BANK * 3], ADD)
+        quantise(3)
         for c in (0, 1):
             nc.scalar.copy(zb[c][:], woven[c])
             quantise(c)
-        read_out(3)
         nc.scalar.copy(zb[2][:, 0:half, :], woven[2][:, 0:half, :])
+        read_out(3)
         quantise(2)
         read_out(0)
         read_out(1)

@@ -343,6 +343,11 @@ def tile_list_woven_probe_lighting_kernel(
 
         nc.gpsimd.tensor_tensor(fourth(3), last[:, BANK * 3 :], hist_sb[PACK - 1][:, BANK * 3 :], ADD)
         add_to_pairs(0, BANK)
+        for k in range(4):
+            nc.tensor.matmul_mx(
+                hist_bank(0), lhsT=w2c[:, 0 : 2 * P].bitcast(FP4X4), lhsT_scale=w2s[:, 0:P],
+                rhs=g2w[:, 0:BANK].bitcast(FP8X4), rhs_scale=g2s[:, 0:BANK], start=True, stop=True,
+            )
         add_to_pairs(1, BANK)
         add_to_pairs(2, half)
         nc.vector.tensor_tensor(fourth(2)[:, half:], hist_bank(2)[:, half:], last[:, BANK * 2 + half : BANK * 3], ADD)

@@ -23,6 +23,8 @@ PACK = 4
 QUAD = 32
 BANK = 512
 AL = 64
+CHUNKS = T2 // BANK
+BLOCKS = BANK // P
 
 
 def tile_list_woven_probe_lighting_kernel(
@@ -33,11 +35,13 @@ def tile_list_woven_probe_lighting_kernel(
     with ExitStack() as ctx:
         lists = ctx.enter_context(tc.tile_pool(name="lists", bufs=1))
         sb = ctx.enter_context(tc.tile_pool(name="sb", bufs=1))
-        shared = ctx.enter_context(tc.tile_pool(name="shared", bufs=1))
-        ps = ctx.enter_context(tc.psum_pool(name="ps", bufs=4))
+        ps = ctx.enter_context(tc.psum_pool(name="ps", bufs=1))
 
         def new_tile(shape, dtype, name, tag=None, bufs=1):
             return sb.tile(shape, dtype, name=name, tag=tag or name, bufs=bufs, align_bytes=AL)
+
+        def new_bank(shape, index):
+            return ps.tile(shape, F32, name=f"bank{index}", tag=f"bank{index}")
 
         def load_list(src, name):
             dst = lists.tile([P, S // 16], U16, name=name)
@@ -45,36 +49,59 @@ def tile_list_woven_probe_lighting_kernel(
             return dst
 
         def load_words(src, name):
-            cols = src.shape[1]
-            dst = new_tile([P, cols], U32, name)
+            dst = new_tile([P, src.shape[1]], U32, name)
             nc.sync.dma_start(dst[:].bitcast(I32), src.rearrange("p n i -> p (n i)").bitcast(I32))
             return dst
 
-        def load_scales(src, name, clear, queue):
-            passes, cols = src.shape[0], src.shape[2]
+        def load_repeated(rows, name):
+            count, cols = rows.shape
             dst = new_tile([P, cols], U8, name)
-            clear.memset(dst[:].bitcast(I32), 0)
+            words = rows.bitcast(I32).unsqueeze(1).to_broadcast([count, P // count, cols // 4])
+            nc.sync.dma_start(dst[:].bitcast(I32), words)
+            return dst
+
+        def new_plane(cols, name):
+            dst = new_tile([P, cols], U8, name)
+            nc.gpsimd.memset(dst[:].bitcast(I32), 0)
+            return dst
+
+        def load_plane(src, name):
+            dst = new_plane(src.shape[1], name)
             for q in range(4):
-                queue.dma_start(
-                    dst[QUAD * q : QUAD * q + 4 * passes, :].bitcast(I32),
-                    src[:, 4 * q : 4 * q + 4, :].bitcast(I32),
-                )
+                nc.sync.dma_start(dst[QUAD * q : QUAD * q + 4, :].bitcast(I32), src[4 * q : 4 * q + 4, :].bitcast(I32))
             return dst
 
-        def load_wg(src, t, name, tag=None):
-            dst = new_tile([P, S], F32, name, tag)
-            rows = src.rearrange("(q t) j -> t q j", t=PACK)
-            for g in (0, 2, 1, 3):
-                nc.sync.dma_start(dst[QUAD * g : QUAD * (g + 1), :], rows[t])
-            return dst
-
-        def load_wg_pairs(src, name):
+        def load_wg(src, page, name):
             dst = new_tile([P, S], F32, name)
-            rows = src.rearrange("(q t) j -> q t j", t=PACK)[:, 0:2, :]
-            for g in range(2):
-                nc.sync.dma_start(dst[64 * g : 64 * (g + 1), :], rows)
+            rows = src.rearrange("(q t) j -> t q j", t=PACK)
+            if page == 0:
+                for e in range(2):
+                    nc.sync.dma_start(dst[e:P:2, :], rows[e].unsqueeze(1).to_broadcast([QUAD, 2, S]))
+            elif page == 2:
+                nc.sync.dma_start(dst[:], rows[2].unsqueeze(1).to_broadcast([QUAD, 4, S]))
+            else:
+                for g in (0, 2, 1, 3):
+                    nc.sync.dma_start(dst[QUAD * g : QUAD * (g + 1), :], rows[3])
             return dst
 
+        def load_rows(src, page, dst):
+            if page < 2:
+                rows = src.rearrange("(h g q t) m -> h t q g m", h=2, g=2, t=PACK)[page]
+                for e in range(2):
+                    nc.sync.dma_start(dst[e:P:2, :], rows[e])
+            elif page == 2:
+                nc.sync.dma_start(dst[:], src.rearrange("(g q t) m -> t q g m", g=4, t=PACK)[2])
+            else:
+                nc.sync.dma_start(dst[:], src.rearrange("(p t) m -> t p m", t=PACK)[3])
+            return dst
+
+        tint_col = tint.rearrange("(r m) -> r m", m=1)
+
+        def load_tint(page):
+            return load_rows(tint_col, page, new_tile([P, 1], F32, f"tint{page}"))
+
+        o1 = load_list(offs, "o1")
+        tabs = load_repeated(tab_scales.rearrange("a q t -> (a q) t"), "tabs")
         o2 = load_list(offs2, "o2")
         tab2s = new_tile([P, T], U8, "tab2s")
         for q in range(4):
@@ -83,71 +110,72 @@ def tile_list_woven_probe_lighting_kernel(
                 tab2_scales[0, 4 * q : 4 * q + 4, :].bitcast(I32).partition_broadcast(QUAD // 4),
             )
         tab2w = load_words(tab2_words[0], "tab2w")
-        o1 = load_list(offs, "o1")
-        tabw = [load_words(tab_words[0], "tabw0")]
-        w2sraw = load_scales(w2_scales, "w2sraw", nc.gpsimd, nc.sync)
         w2raw = new_tile([P, 2 * H], U8, "w2raw")
         nc.sync.dma_start(w2raw[:].bitcast(I32), w2_words[0].bitcast(I32))
-        tabw.append(load_words(tab_words[1], "tabw1"))
-        tabs = load_scales(tab_scales, "tabs", nc.gpsimd, nc.sync)
-        tint_lo = []
-        for h in range(2):
-            col = new_tile([P, 1], F32, f"tint_lo{h}")
-            nc.sync.dma_start(col[:], tint[256 * h : 256 * (h + 1)].rearrange("(q t) -> q t", t=PACK)[:, 0:2])
-            tint_lo.append(col)
+        w2sraw = load_plane(w2_scales[0], "w2sraw")
+        tabw = [load_words(tab_words[a], f"tabw{a}") for a in range(2)]
+        wg2_pairs = load_wg(wg2, 0, "wg2_pairs")
+        tints = [load_tint(0)]
         o4 = load_list(offs4, "o4")
-        wg2_pairs = load_wg_pairs(wg2, "wg2_pairs")
         w1raw = []
         for a in range(2):
             raw = new_tile([P, PACK, H], F32, f"w1raw{a}")
             nc.sync.dma_start(raw[:], w1[512 * a : 512 * (a + 1), :].rearrange("(p j) c -> p j c", j=PACK))
             w1raw.append(raw)
-        tint_hi = new_tile([P, PACK], F32, "tint_hi")
-        nc.sync.dma_start(tint_hi[:], tint.rearrange("(p t) -> p t", t=PACK))
-        tints = [tint_lo[0][:], tint_lo[1][:], tint_hi[:, 2:3], tint_hi[:, 3:4]]
-        wg2_sb = [wg2_pairs, wg2_pairs, load_wg(wg2, 2, "wg2_2")]
-        o3 = load_list(offs3, "o3")
-        wg1_pairs = load_wg_pairs(wg1, "wg1_pairs")
-        hist_sb = []
-        for t, tag in enumerate(("hist0", "tab2w", "tabw0", "tabw1")):
-            rows = new_tile([P, T2], F32, f"hist{t}", tag)
-            if t < 2:
-                src = hist[256 * t : 256 * (t + 1), :].rearrange("(q t) m -> q t m", t=PACK)[:, 0:2, :]
-            else:
-                src = hist.rearrange("(p t) m -> t p m", t=PACK)[t]
-            nc.sync.dma_start(rows[:], src)
-            hist_sb.append(rows)
-        wg1_sb = [wg1_pairs, wg1_pairs, load_wg(wg1, 2, "wg1_2"), load_wg(wg1, 3, "wg1_3")]
-        wbw = load_words(wb_words[0], "wbw")
-        wbs = load_scales(wb_scales, "wbs", nc.gpsimd, nc.sync)
-        ident0 = new_tile([P, P], F32, "ident0")
-        make_identity(nc, ident0[:])
+            tints.append(load_tint(1 + a))
+        g1s = new_plane(S, "g1s")
+        ident = new_tile([P, P], F32, "ident")
+        make_identity(nc, ident[:])
 
+        g1rows = new_tile([P, S], U8, "g1rows")
+        nc.vector.tensor_copy(g1rows[:], tabs[:].indirect(o1[:]))
         g2s = new_tile([P, S], U8, "g2s")
         nc.vector.tensor_copy(g2s[:], tab2s[:].indirect(o2[:]))
         g2w = new_tile([P, S], U32, "g2w")
         nc.vector.tensor_copy(g2w[:], tab2w[:].indirect(o2[:]))
         g1w = new_tile([P, 2, S], U32, "g1w")
-        nc.vector.tensor_copy(g1w[:, 0, :], tabw[0][:].indirect(o1[:]))
+        for a in range(2):
+            nc.vector.tensor_copy(g1w[:, a, :], tabw[a][:].indirect(o1[:]))
+        for a in range(2):
+            for r in range(4):
+                nc.sync.dma_start(
+                    g1s[4 * a + r : P : QUAD, :].bitcast(I32),
+                    g1rows[64 * a + 4 * r : 64 * (a + 1) : 16, :].bitcast(I32),
+                )
+
+        tints.append(load_tint(3))
+        wg2_sb = [wg2_pairs, wg2_pairs, load_wg(wg2, 2, "wg2_2")]
+        o3 = load_list(offs3, "o3")
+        wg1_third = load_wg(wg1, 2, "wg1_2")
+        wg1_pairs = load_wg(wg1, 0, "wg1_pairs")
+        wg1_sb = [wg1_pairs, wg1_pairs, wg1_third]
+        hist_sb = {}
+        for t, tag in ((2, "hist2"), (0, "tab2w"), (3, "tabw0")):
+            hist_sb[t] = load_rows(hist, t, new_tile([P, T2], F32, f"hist{t}", tag))
+        wbw = load_words(wb_words[0], "wbw")
+        wbs = load_plane(wb_scales[0], "wbs")
+        wg2_sb.append(load_wg(wg2, 3, "wg2_3"))
+        waraw = new_tile([P, PACK, N], F32, "waraw")
+        nc.sync.dma_start(waraw[:], wa.rearrange("(p j) c -> p j c", j=PACK))
+        hist_sb[1] = load_rows(hist, 1, new_tile([P, T2], F32, "hist1", "tabw1"))
+        wg1_sb.append(load_wg(wg1, 3, "wg1_3"))
 
         w2c = new_tile([P, 2 * H], U8, "w2c")
         w2s = new_tile([P, H], U8, "w2s")
-        nc.gpsimd.tensor_copy(w2c[:, 0:H].bitcast(U32), w2raw[:].bitcast(U32).rearrange("p (q u) -> p q u", u=2)[:, :, 0])
-        nc.gpsimd.tensor_copy(
-            w2s[:, 0 : H // 2].rearrange("p (q e) -> p q e", e=2),
-            w2sraw[:].rearrange("p (q t) -> p q t", t=PACK)[:, :, 0:2],
+        nc.scalar.copy(
+            w2c[:, 0:H].bitcast(U32).rearrange("p (h q g) -> p h q g", h=2, g=2),
+            w2raw[:].bitcast(U32).rearrange("p (h g q u) -> p h q g u", h=2, g=2, u=2)[:, :, :, :, 0],
         )
-        nc.gpsimd.tensor_copy(
-            w2c[:, H : 2 * H].rearrange("p (t m b) -> p t m b", t=2, b=2),
-            w2raw[:].rearrange("p (m t b) -> p t m b", t=PACK, b=2)[:, 2:4, :, :],
+        nc.scalar.copy(
+            w2s[:, 0 : H // 2].bitcast(U16).rearrange("p (h q g) -> p h q g", h=2, g=2),
+            w2sraw[:].bitcast(U16).rearrange("p (h g q u) -> p h q g u", h=2, g=2, u=2)[:, :, :, :, 0],
         )
-        nc.gpsimd.tensor_copy(
-            w2s[:, H // 2 : H].rearrange("p (t m) -> p t m", t=2),
-            w2sraw[:].rearrange("p (m t) -> p t m", t=PACK)[:, 2:4, :],
-        )
-        nc.vector.tensor_copy(g1w[:, 1, :], tabw[1][:].indirect(o1[:]))
-        g1s = new_tile([P, S], U8, "g1s")
-        nc.vector.tensor_copy(g1s[:], tabs[:].indirect(o1[:]))
+        w2half = w2raw[:].bitcast(U16).rearrange("p (g q t) -> p t q g", g=4, t=PACK)
+        w2byte = w2sraw[:].rearrange("p (g q t) -> p t q g", g=4, t=PACK)
+        nc.scalar.copy(w2c[:, H : H + 2 * P].bitcast(U16).rearrange("p (q g) -> p q g", g=4), w2half[:, 2])
+        nc.scalar.copy(w2c[:, H + 2 * P :].bitcast(U16).rearrange("p (g q) -> p q g", g=4), w2half[:, 3])
+        nc.gpsimd.tensor_copy(w2s[:, 2 * P : 3 * P].rearrange("p (q g) -> p q g", g=4), w2byte[:, 2])
+        nc.gpsimd.tensor_copy(w2s[:, 3 * P :].rearrange("p (g q) -> p q g", g=4), w2byte[:, 3])
 
         page = [new_tile([P, T2], F32, f"page{t}") for t in range(PACK)]
         h1 = [new_tile([P, S], F32, f"h1_{t}") for t in range(PACK)]
@@ -156,9 +184,10 @@ def tile_list_woven_probe_lighting_kernel(
 
         def glossy(t):
             h2.append(new_tile([P, S], F32, f"h2_{t}", h2_tags[t]))
+            linear = new_tile([P, S], F32, "linear")
             for b in range(2):
                 cols = slice(BANK * b, BANK * (b + 1))
-                acc = ps.tile([P, BANK], F32, name="acc", tag="mm")
+                acc = new_bank([P, BANK], (2 * t + b) % 4)
                 nc.tensor.matmul_mx(
                     acc[:],
                     lhsT=w2c[:, 2 * P * t : 2 * P * (t + 1)].bitcast(FP4X4),
@@ -167,10 +196,10 @@ def tile_list_woven_probe_lighting_kernel(
                     rhs_scale=g2s[:, cols],
                     start=True, stop=True,
                 )
-                nc.scalar.activation(h2[t][:, cols], acc[:], ACT.Exp)
+                nc.scalar.activation(linear[:, cols], acc[:], ACT.Exp)
             for b in range(2):
                 cols = slice(BANK * b, BANK * (b + 1))
-                nc.scalar.activation(h2[t][:, cols], h2[t][:, cols], ACT.Copy, scale=tints[t])
+                nc.scalar.activation(h2[t][:, cols], linear[:, cols], ACT.Copy, scale=tints[t][:])
 
         def scatter(t, places, h, wg):
             nc.vector.tensor_tensor(page[t][:].indirect(places[:]), h[t][:], wg[t][:], MULT)
@@ -181,12 +210,12 @@ def tile_list_woven_probe_lighting_kernel(
 
         w1b = new_tile([P, 2, PACK, P, PACK], BF16, "w1b")
         for a in range(2):
-            by_four = w1raw[a][:].rearrange("p j (m t) -> p m t j", t=PACK)
-            nc.scalar.copy(
-                w1b[:, a, 0:2, :, :].rearrange("p h (q e) j -> p (h q) e j", e=2),
-                by_four[:, :, 0:2, :],
-            )
-            nc.scalar.copy(w1b[:, a, 2:4, :, :].rearrange("p t m j -> p m t j"), by_four[:, :, 2:4, :])
+            by_pair = w1raw[a][:].rearrange("p j (h g q t) -> p h q g t j", h=2, g=2, t=PACK)
+            by_row = w1raw[a][:].rearrange("p j (g q t) -> p t q g j", g=4, t=PACK)
+            for h in range(2):
+                nc.scalar.copy(w1b[:, a, h].rearrange("p (q g e) j -> p q g e j", g=2, e=2), by_pair[:, h, :, :, 0:2, :])
+            nc.scalar.copy(w1b[:, a, 2].rearrange("p (q g) j -> p q g j", g=4), by_row[:, 2])
+            nc.scalar.copy(w1b[:, a, 3].rearrange("p (g q) j -> p q g j", g=4), by_row[:, 3])
         w1c = new_tile([P, PACK * 2 * P], U32, "w1c")
         w1s = new_tile([P, PACK * 2 * P], U8, "w1s")
         nc.vector.quantize_mx(w1c[:].bitcast(FP8X4), w1s[:], w1b[:].rearrange("p a t m j -> p (a t m j)"))
@@ -194,10 +223,10 @@ def tile_list_woven_probe_lighting_kernel(
         glossy(2)
         scatter(2, o4, h2, wg2_sb)
 
-        for t in range(PACK):
+        for t in (2, 0, 1, 3):
             for b in range(2):
                 cols = slice(BANK * b, BANK * (b + 1))
-                acc = ps.tile([P, BANK], F32, name="acc", tag="mm")
+                acc = new_bank([P, BANK], (2 * t + b) % 4)
                 for a in range(2):
                     wcols = slice(P * (PACK * a + t), P * (PACK * a + t + 1))
                     nc.tensor.matmul_mx(
@@ -210,154 +239,171 @@ def tile_list_woven_probe_lighting_kernel(
                     )
                 nc.scalar.activation(h1[t][:, cols], acc[:], ACT.Relu)
 
-        ident = new_tile([P, P], F32, "ident", "g1s")
-        nc.scalar.copy(ident[:], ident0[:])
         glossy(3)
         warm = new_tile([P, 1], F32, "warm")
         nc.scalar.activation(warm[:], h2[PACK - 1][:, S - 1 : S], ACT.Sigmoid)
 
-        for t in range(PACK - 1):
+        for t in (2, 0, 1):
             scatter(t, o3, h1, wg1_sb)
-        wg2_last = new_tile([P, S], F32, "wg2_3", "wg1_pairs")
-        wg2_rows = wg2.rearrange("(q t) j -> t q j", t=PACK)[PACK - 1]
-        for g in (0, 2, 1):
-            nc.sync.dma_start(wg2_last[QUAD * g : QUAD * (g + 1), :], wg2_rows)
-        waraw = new_tile([P, PACK, N], F32, "waraw", "h1_1")
-        nc.sync.dma_start(waraw[:], wa.rearrange("(p j) c -> p j c", j=PACK))
-        nc.sync.dma_start(wg2_last[QUAD * 3 :, :], wg2_rows)
-        wg2_sb.append(wg2_last)
         scatter(PACK - 1, o4, h2, wg2_sb)
-        scatter(PACK - 1, o3, h1, wg1_sb)
         wab = new_tile([P, N, PACK], BF16, "wab")
         nc.scalar.copy(wab[:], waraw[:].rearrange("p j n -> p n j"))
         wac = new_tile([P, N], U32, "wac")
         was = new_tile([P, N], U8, "was")
         nc.vector.quantize_mx(wac[:].bitcast(FP8X4), was[:], wab[:].rearrange("p n j -> p (n j)"))
+        scatter(PACK - 1, o3, h1, wg1_sb)
 
+        on_vector = (0, 1)
+        first, second = 2, 3
+        ring = [0]
 
-        chunks = T2 // BANK
-        blocks = BANK // P
-        zt_all = shared.tile([P, chunks, blocks, P, 2], BF16, name="zt_all", align_bytes=AL, offset=2048)
-        zt = [zt_all[:, c, :, :, :] for c in range(chunks)]
-        pairs = [new_tile([P, 2, BANK], F32, f"pairs{c}") for c in range(chunks)]
+        def next_bank(shape):
+            ring[0] = (ring[0] + 1) % 4
+            return new_bank(shape, 4 + ring[0])
 
-        def add_turned(t, c):
-            bank = ps.tile([P, blocks, P], F32, name="bank", tag="tr")
-            for blk in range(blocks):
-                cols = slice(BANK * c + P * blk, BANK * c + P * (blk + 1))
-                nc.tensor.matmul(bank[:, blk, :], lhsT=hist_sb[t][:, cols], rhs=ident[:], is_transpose=True, start=True, stop=False)
-                nc.tensor.matmul(bank[:, blk, :], lhsT=page[t][:, cols], rhs=ident[:], is_transpose=True, start=False, stop=True)
-            nc.scalar.copy(zt[c].rearrange("m b p e -> m b (p e)")[:, :, P * t : P * (t + 1)], bank[:])
+        def block(c, blk):
+            return slice(BANK * c + P * blk, BANK * c + P * (blk + 1))
 
-        def turn_back(u, c):
-            bank = ps.tile([P, blocks, P], F32, name="bank", tag="tr")
-            words = zt[c].rearrange("m b p e -> m (b p e)").bitcast(F32)
-            for blk in range(blocks):
-                nc.tensor.transpose(bank[:, blk, :], words[:, P * blk : P * (blk + 1)], ident[:])
-            nc.scalar.copy(pairs[c][:, u, :], bank[:].rearrange("p b m -> p (b m)"))
+        def turned_sum(t, c):
+            bank = next_bank([P, BLOCKS, P])
+            for blk in range(BLOCKS):
+                nc.tensor.matmul(bank[:, blk, :], lhsT=hist_sb[t][:, block(c, blk)], rhs=ident[:], is_transpose=True, start=True, stop=False)
+                nc.tensor.matmul(bank[:, blk, :], lhsT=page[t][:, block(c, blk)], rhs=ident[:], is_transpose=True, start=False, stop=True)
+            return bank
 
-        on_vector = (0, 1, 2)
+        def words(zt, blk):
+            return zt[:].rearrange("m b p e -> m (b p e)").bitcast(F32)[:, P * blk : P * (blk + 1)]
+
+        pieces = ((0, 0, BANK // 2), (0, BANK // 2, BANK), (1, 0, BANK))
+        pairs = [new_tile([P, 2, hi - lo], F32, f"pairs{i}") for i, (c, lo, hi) in enumerate(pieces)]
+
+        def turn_back(zt, u, c, bank):
+            for blk in range(BLOCKS):
+                nc.tensor.transpose(bank[:, P * blk : P * (blk + 1)], words(zt, blk), ident[:])
+            for i, (chunk, lo, hi) in enumerate(pieces):
+                if chunk == c:
+                    nc.scalar.copy(pairs[i][:, u, :], bank[:, lo:hi])
+
+        high = [new_tile([P, BLOCKS, P, 2], BF16, f"high{c}") for c in range(CHUNKS)]
+        for c in range(CHUNKS):
+            bank = turned_sum(2, c)
+            nc.scalar.copy(
+                high[c][:].rearrange("m b (g q) e -> m b g q e", g=4),
+                bank[:].rearrange("m b (q g) -> m b g q", g=4).unsqueeze(4).to_broadcast([P, BLOCKS, 4, QUAD, 2]),
+            )
+        for c in on_vector:
+            turn_back(high[c], 1, c, next_bank([P, BANK]))
+
+        low = [new_tile([P, BLOCKS, P, 2], BF16, f"low{c}") for c in range(CHUNKS)]
+
+        def round_pairs(t, c, bank):
+            nc.scalar.copy(
+                low[c][:, :, 64 * t : 64 * (t + 1), :].rearrange("m b (g q) e -> m b g q e", g=2),
+                bank[:].rearrange("m b (q g e) -> m b g q e", g=2, e=2),
+            )
+
+        for c in range(CHUNKS):
+            round_pairs(0, c, turned_sum(0, c))
         hist_t = new_tile([P, len(on_vector), BANK], F32, "hist_t", "w1raw0")
-        for i, c in enumerate(on_vector):
-            bank = ps.tile([P, blocks, P], F32, name="bank", tag="tr")
-            for blk in range(blocks):
-                cols = slice(BANK * c + P * blk, BANK * c + P * (blk + 1))
-                nc.tensor.transpose(bank[:, blk, :], hist_sb[PACK - 1][:, cols], ident[:])
-            nc.scalar.copy(hist_t[:, i, :], bank[:].rearrange("m b p -> m (b p)"))
+        hist_ps = []
+        for c in on_vector:
+            bank = next_bank([P, BLOCKS, P])
+            for blk in range(BLOCKS):
+                nc.tensor.transpose(bank[:, blk, :], hist_sb[PACK - 1][:, block(c, blk)], ident[:])
+            nc.scalar.copy(hist_t[:, c, :], bank[:].rearrange("m b p -> m (b p)"))
+        held = [new_bank([P, BLOCKS, P], c) for c in range(CHUNKS)]
+        for c in range(CHUNKS):
+            for blk in range(BLOCKS):
+                nc.tensor.matmul(held[c][:, blk, :], lhsT=hist_sb[1][:, block(c, blk)], rhs=ident[:], is_transpose=True, start=(blk == 0), stop=False)
+        for c in range(CHUNKS):
+            for blk in range(BLOCKS):
+                nc.tensor.matmul(held[c][:, blk, :], lhsT=page[1][:, block(c, blk)], rhs=ident[:], is_transpose=True, start=False, stop=(blk == BLOCKS - 1))
+            round_pairs(1, c, held[c])
+        for c in on_vector:
+            turn_back(low[c], 0, c, new_bank([P, BANK], 4 + c))
 
-        for t in range(2):
-            for c in range(chunks):
-                add_turned(t, c)
-        for c in range(chunks):
-            turn_back(0, c)
-        held = []
-        for c in range(chunks):
-            bank = ps.tile([P, blocks, P], F32, name="held", tag="mm")
-            for blk in range(blocks):
-                cols = slice(BANK * c + P * blk, BANK * c + P * (blk + 1))
-                nc.tensor.matmul(bank[:, blk, :], lhsT=hist_sb[2][:, cols], rhs=ident[:], is_transpose=True, start=(blk == 0), stop=False)
-            held.append(bank)
-        for c in range(chunks):
-            for blk in range(blocks):
-                cols = slice(BANK * c + P * blk, BANK * c + P * (blk + 1))
-                nc.tensor.matmul(held[c][:, blk, :], lhsT=page[2][:, cols], rhs=ident[:], is_transpose=True, start=False, stop=(blk == blocks - 1))
-            nc.scalar.copy(zt[c][:, :, :, 0], held[c][:])
-        hist_ps = {}
-        for i, c in enumerate(on_vector):
-            bank = ps.tile([P, blocks, P], F32, name="hist_ps", tag="mm")
-            for blk in range(blocks):
-                nc.tensor.transpose(bank[:, blk, :], hist_t[:, i, P * blk : P * (blk + 1)], ident[:])
-            hist_ps[c] = bank
-        free_tags = h2_tags + [f"h1_{t}" for t in range(PACK)]
-        zb = [shared.tile([P, BANK, 2], F32, name=f"zb{c}", align_bytes=AL, offset=4096 * c) for c in range(chunks)]
-        woven = [pairs[c][:].rearrange("p u m -> p m u") for c in range(chunks)]
-        z = [(new_tile([P, BANK], U32, f"zc{c}"), new_tile([P, BANK], U8, f"zs{c}")) for c in range(chunks)]
+        zb = [new_tile([P, BANK, 2], F32, f"zb{c}", tag)[:] for c, tag in enumerate(("low2", "high2", "tab2w", "hist2"))]
+
+        def turn_both(c, blocks, bank):
+            for u, zt in enumerate((low[c], high[c])):
+                for i, blk in enumerate(blocks):
+                    nc.tensor.transpose(bank[:, u, P * i : P * (i + 1)], words(zt, blk), ident[:])
+
+        def weave(c, blocks, bank):
+            nc.scalar.copy(zb[c][:, P * blocks[0] : P * (blocks[-1] + 1), :], bank[:].rearrange("p u m -> p m u"))
+
+        for c, blocks, index in ((second, (0, 1), 6), (second, (2,), 7), (first, (0, 1), 4), (first, (2, 3), 5)):
+            bank = new_bank([P, 2, P * len(blocks)], index)
+            turn_both(c, blocks, bank)
+            weave(c, blocks, bank)
+        for (c, lo, hi), index in zip(pieces, (6, 7, 4)):
+            bank = new_bank([P, hi - lo], index)
+            for at in range(lo, hi, P):
+                nc.tensor.transpose(bank[:, at - lo : at - lo + P], hist_t[:, c, at : at + P], ident[:])
+            hist_ps.append(bank)
+
+        z = {}
+        free_tags = ["h2_0", "h2_1", "linear", "w1b", "h1_0", "h1_1", "h1_2", "h1_3"]
         last = page[PACK - 1]
 
-        def hist_bank(c):
-            return hist_ps[c][:].rearrange("p b m -> p (b m)")
+        def rounded(c):
+            return zb[c].rearrange("p m u -> p (m u)").bitcast(BF16)
 
-        def fourth(c):
-            return zb[c][:].rearrange("p m u -> p (m u)").bitcast(BF16).rearrange("p (m j) -> p m j", j=PACK)[:, :, PACK - 1]
+        def add_in_place(c):
+            cols = slice(BANK * c, BANK * (c + 1))
+            fourth = rounded(c).rearrange("p (m j) -> p m j", j=PACK)[:, :, PACK - 1]
+            nc.gpsimd.tensor_tensor(fourth, last[:, cols], hist_sb[PACK - 1][:, cols], ADD)
+
+        def add_to_pairs(i):
+            c, lo, hi = pieces[i]
+            halves = pairs[i][:, 1, :].bitcast(BF16).rearrange("p (m e) -> p m e", e=2)
+            nc.vector.tensor_tensor(halves[:, :, 1], hist_ps[i][:], last[:, BANK * c + lo : BANK * c + hi], ADD)
 
         def quantise(c):
-            nc.vector.quantize_mx(z[c][0][:].bitcast(FP8X4), z[c][1][:], zb[c][:].rearrange("p m u -> p (m u)").bitcast(BF16))
+            z[c] = (new_tile([P, BANK], U32, f"zc{c}"), new_tile([P, BANK], U8, f"zs{c}"))
+            nc.vector.quantize_mx(z[c][0][:].bitcast(FP8X4), z[c][1][:], rounded(c))
 
-
-        def product(c, name, tag, wc, ws, n):
-            acc = ps.tile([P, BANK], F32, name=name, tag=tag)
+        def read_out(turn, c, n):
             rows = slice(P * n, P * (n + 1))
+            sums = []
+            for wc, ws, banks in ((wbw, wbs, (0, 1, 2, 3)), (wac, was, (5, 7, 6, 4))):
+                acc = new_bank([P, BANK], banks[turn % 4])
+                nc.tensor.matmul_mx(
+                    acc[:], lhsT=wc[:, rows].bitcast(FP8X4), lhsT_scale=ws[:, rows],
+                    rhs=z[c][0][:].bitcast(FP8X4), rhs_scale=z[c][1][:], start=True, stop=True,
+                )
+                sums.append(acc)
+            gate = new_tile([P, BANK], F32, f"gate{turn}", f"zc{second}" if turn == 2 else None)
+            nc.scalar.activation(gate[:], sums[0][:], ACT.Sigmoid)
+            res = new_tile([P, BANK], F32, "res", free_tags[turn])
+            width = BANK // 2 if turn == 2 * CHUNKS - 1 else BANK
+            for lo in range(0, BANK, width):
+                part = slice(lo, lo + width)
+                nc.vector.tensor_tensor(res[:, part], sums[1][:, part], gate[:, part], MULT)
+                nc.sync.dma_start(out[rows, BANK * c + lo : BANK * c + lo + width], res[:, part])
+
+        add_in_place(first)
+        add_to_pairs(0)
+        warm_bank = new_bank([P, BANK], 6)
+        for k in range(3):
             nc.tensor.matmul_mx(
-                acc[:], lhsT=wc[:, rows].bitcast(FP8X4), lhsT_scale=ws[:, rows],
-                rhs=z[c][0][:].bitcast(FP8X4), rhs_scale=z[c][1][:], start=True, stop=True,
-            )
-            return acc
-
-        def read_out(c, final=False):
-            if final:
-                vis = [product(c, "vis", "mm", wbw, wbs, n) for n in range(N // P)]
-                light = [product(c, "light", "tr", wac, was, n) for n in range(N // P)]
-            else:
-                both = [(product(c, "vis", "mm", wbw, wbs, n), product(c, "light", "tr", wac, was, n)) for n in range(N // P)]
-                vis, light = zip(*both)
-            for n in range(N // P):
-                gate = new_tile([P, BANK], F32, "gate", bufs=3)
-                nc.scalar.activation(gate[:], vis[n][:], ACT.Sigmoid)
-                res = new_tile([P, BANK], F32, "res", free_tags[2 * c + n])
-                width = BANK // 2 if final and n == N // P - 1 else BANK
-                for lo in range(0, BANK, width):
-                    part = slice(lo, lo + width)
-                    nc.vector.tensor_tensor(res[:, part], light[n][:, part], gate[:, part], MULT)
-                    nc.sync.dma_start(out[P * n : P * (n + 1), BANK * c + lo : BANK * c + lo + width], res[:, part])
-
-        def add_to_pairs(c, width):
-            halves = pairs[c][:, 1, :].bitcast(BF16).rearrange("p (m e) -> p m e", e=2)
-            nc.vector.tensor_tensor(halves[:, 0:width, 1], hist_bank(c)[:, 0:width], last[:, BANK * c : BANK * c + width], ADD)
-
-        half = BANK // 2
-        turn_back(1, 3)
-        nc.scalar.copy(zb[3][:], woven[3])
-        for c in range(3):
-            turn_back(1, c)
-        nc.scalar.copy(zb[2][:, half:, :], woven[2][:, half:, :])
-
-        nc.gpsimd.tensor_tensor(fourth(3), last[:, BANK * 3 :], hist_sb[PACK - 1][:, BANK * 3 :], ADD)
-        add_to_pairs(0, BANK)
-        for k in range(4):
-            nc.tensor.matmul_mx(
-                hist_bank(0), lhsT=w2c[:, 0 : 2 * P].bitcast(FP4X4), lhsT_scale=w2s[:, 0:P],
+                warm_bank[:], lhsT=w2c[:, 0 : 2 * P].bitcast(FP4X4), lhsT_scale=w2s[:, 0:P],
                 rhs=g2w[:, 0:BANK].bitcast(FP8X4), rhs_scale=g2s[:, 0:BANK], start=True, stop=True,
             )
-        add_to_pairs(1, BANK)
-        add_to_pairs(2, half)
-        nc.vector.tensor_tensor(fourth(2)[:, half:], hist_bank(2)[:, half:], last[:, BANK * 2 + half : BANK * 3], ADD)
-        quantise(3)
-        for c in (0, 1):
-            nc.scalar.copy(zb[c][:], woven[c])
+        add_to_pairs(1)
+        add_to_pairs(2)
+        tail_bank = new_bank([P, 2, P], 4)
+        turn_both(second, (BLOCKS - 1,), tail_bank)
+        for i, (c, lo, hi) in enumerate(pieces):
+            nc.scalar.copy(zb[c][:, lo:hi, :], pairs[i][:].rearrange("p u m -> p m u"))
+        for c in (0, first, 1):
             quantise(c)
-        nc.scalar.copy(zb[2][:, 0:half, :], woven[2][:, 0:half, :])
-        read_out(3)
-        quantise(2)
-        read_out(0)
-        read_out(1)
-        read_out(2, final=True)
+        read_out(0, 0, 0)
+        weave(second, (BLOCKS - 1,), tail_bank)
+        add_in_place(second)
+        read_out(1, 0, 1)
+        read_out(2, first, 0)
+        read_out(3, first, 1)
+        quantise(second)
+        for turn, (c, n) in enumerate(((1, 0), (1, 1), (second, 0), (second, 1)), 4):
+            read_out(turn, c, n)

@@ -274,15 +274,19 @@ def tile_list_woven_probe_lighting_kernel(
         def words(zt, blk):
             return zt[:].rearrange("m b p e -> m (b p e)").bitcast(F32)[:, P * blk : P * (blk + 1)]
 
-        pieces = ((0, 0, BANK // 2), (0, BANK // 2, BANK), (1, 0, BANK))
-        pairs = [new_tile([P, 2, hi - lo], F32, f"pairs{i}") for i, (c, lo, hi) in enumerate(pieces)]
+        half = BANK // 2
+        lead = 16
+        pieces = ((0, 0, half), (1, 0, half), (1, half, BANK))
+        pairs = [new_tile([P, 2, half + (lead if i == 2 else 0)], F32, f"pairs{i}") for i in range(len(pieces))]
 
         def turn_back(zt, u, c, bank):
-            for blk in range(BLOCKS):
-                nc.tensor.transpose(bank[:, P * blk : P * (blk + 1)], words(zt, blk), ident[:])
             for i, (chunk, lo, hi) in enumerate(pieces):
                 if chunk == c:
-                    nc.scalar.copy(pairs[i][:, u, :], bank[:, lo:hi])
+                    for at in range(lo, hi, P):
+                        nc.tensor.transpose(bank[:, at : at + P], words(zt, at // P), ident[:])
+            for i, (chunk, lo, hi) in enumerate(pieces):
+                if chunk == c:
+                    nc.scalar.copy(pairs[i][:, u, 0:half], bank[:, lo:hi])
 
         high = [new_tile([P, BLOCKS, P, 2], BF16, f"high{c}") for c in range(CHUNKS)]
         for c in range(CHUNKS):
@@ -305,7 +309,6 @@ def tile_list_woven_probe_lighting_kernel(
         for c in range(CHUNKS):
             round_pairs(0, c, turned_sum(0, c))
         hist_t = new_tile([P, len(on_vector), BANK], F32, "hist_t", "w1raw0")
-        hist_ps = []
         for c in on_vector:
             bank = next_bank([P, BLOCKS, P])
             for blk in range(BLOCKS):
@@ -322,25 +325,25 @@ def tile_list_woven_probe_lighting_kernel(
         for c in on_vector:
             turn_back(low[c], 0, c, new_bank([P, BANK], 4 + c))
 
-        zb = [new_tile([P, BANK, 2], F32, f"zb{c}", tag)[:] for c, tag in enumerate(("low2", "high2", "tab2w", "hist2"))]
+        late = new_tile([P, 2 * BANK, 2], F32, "late", "hist2")
+        zb = [new_tile([P, BANK, 2], F32, "zb0", "w1raw1")[:], late[:, 0:BANK, :], new_tile([P, BANK, 2], F32, "zb2", "tab2w")[:], late[:, BANK:, :]]
 
-        def turn_both(c, blocks, bank):
+        for c, lo, index in ((0, half, 6), (second, 0, 7), (second, half, 0), (first, 0, 1), (first, half, 2)):
+            bank = new_bank([P, 2, half], index)
             for u, zt in enumerate((low[c], high[c])):
-                for i, blk in enumerate(blocks):
-                    nc.tensor.transpose(bank[:, u, P * i : P * (i + 1)], words(zt, blk), ident[:])
-
-        def weave(c, blocks, bank):
-            nc.scalar.copy(zb[c][:, P * blocks[0] : P * (blocks[-1] + 1), :], bank[:].rearrange("p u m -> p m u"))
-
-        for c, blocks, index in ((second, (0, 1), 6), (second, (2,), 7), (first, (0, 1), 4), (first, (2, 3), 5)):
-            bank = new_bank([P, 2, P * len(blocks)], index)
-            turn_both(c, blocks, bank)
-            weave(c, blocks, bank)
-        for (c, lo, hi), index in zip(pieces, (6, 7, 4)):
+                for at in range(0, half, P):
+                    nc.tensor.transpose(bank[:, u, at : at + P], words(zt, (lo + at) // P), ident[:])
+            skip = lead if (c, lo) == (second, 0) else 0
+            if skip:
+                nc.scalar.copy(pairs[2][:, :, half:], bank[:, :, 0:skip])
+            nc.scalar.copy(zb[c][:, lo + skip : lo + half, :], bank[:, :, skip:].rearrange("p u m -> p m u"))
+        hist_ps = {}
+        for c, lo, hi, index in ((0, 0, half, 7), (0, half, BANK, 0), (1, 0, BANK, 1)):
             bank = new_bank([P, hi - lo], index)
             for at in range(lo, hi, P):
                 nc.tensor.transpose(bank[:, at - lo : at - lo + P], hist_t[:, c, at : at + P], ident[:])
-            hist_ps.append(bank)
+            for at in range(lo, hi, half):
+                hist_ps[c, at] = bank[:, at - lo : at - lo + half]
 
         z = {}
         free_tags = ["h2_0", "h2_1", "linear", "w1b", "h1_0", "h1_1", "h1_2", "h1_3"]
@@ -349,31 +352,37 @@ def tile_list_woven_probe_lighting_kernel(
         def rounded(c):
             return zb[c].rearrange("p m u -> p (m u)").bitcast(BF16)
 
+        def fourth(c):
+            return rounded(c).rearrange("p (m j) -> p m j", j=PACK)[:, :, PACK - 1]
+
         def add_in_place(c):
             cols = slice(BANK * c, BANK * (c + 1))
-            fourth = rounded(c).rearrange("p (m j) -> p m j", j=PACK)[:, :, PACK - 1]
-            nc.gpsimd.tensor_tensor(fourth, last[:, cols], hist_sb[PACK - 1][:, cols], ADD)
+            nc.gpsimd.tensor_tensor(fourth(c), last[:, cols], hist_sb[PACK - 1][:, cols], ADD)
 
         def add_to_pairs(i):
             c, lo, hi = pieces[i]
-            halves = pairs[i][:, 1, :].bitcast(BF16).rearrange("p (m e) -> p m e", e=2)
-            nc.vector.tensor_tensor(halves[:, :, 1], hist_ps[i][:], last[:, BANK * c + lo : BANK * c + hi], ADD)
+            halves = pairs[i][:, 1, 0:half].bitcast(BF16).rearrange("p (m e) -> p m e", e=2)
+            nc.vector.tensor_tensor(halves[:, :, 1], hist_ps[c, lo], last[:, BANK * c + lo : BANK * c + hi], ADD)
 
-        def quantise(c):
-            z[c] = (new_tile([P, BANK], U32, f"zc{c}"), new_tile([P, BANK], U8, f"zs{c}"))
+        def quantise(c, tag):
+            z[c] = (new_tile([P, BANK], U32, f"zc{c}", f"zc{tag}"), new_tile([P, BANK], U8, f"zs{c}"))
             nc.vector.quantize_mx(z[c][0][:].bitcast(FP8X4), z[c][1][:], rounded(c))
 
-        def read_out(turn, c, n):
+        def multiply(turn, c, n):
             rows = slice(P * n, P * (n + 1))
             sums = []
-            for wc, ws, banks in ((wbw, wbs, (0, 1, 2, 3)), (wac, was, (5, 7, 6, 4))):
+            for wc, ws, banks in ((wbw, wbs, (2, 3, 4, 5)), (wac, was, (6, 0, 1, 7))):
                 acc = new_bank([P, BANK], banks[turn % 4])
                 nc.tensor.matmul_mx(
                     acc[:], lhsT=wc[:, rows].bitcast(FP8X4), lhsT_scale=ws[:, rows],
                     rhs=z[c][0][:].bitcast(FP8X4), rhs_scale=z[c][1][:], start=True, stop=True,
                 )
                 sums.append(acc)
-            gate = new_tile([P, BANK], F32, f"gate{turn}", f"zc{second}" if turn == 2 else None)
+            return sums
+
+        def read_out(turn, c, n, sums):
+            rows = slice(P * n, P * (n + 1))
+            gate = new_tile([P, BANK], F32, f"gate{turn}", f"zc{second}" if turn == 1 else None)
             nc.scalar.activation(gate[:], sums[0][:], ACT.Sigmoid)
             res = new_tile([P, BANK], F32, "res", free_tags[turn])
             width = BANK // 2 if turn == 2 * CHUNKS - 1 else BANK
@@ -384,26 +393,28 @@ def tile_list_woven_probe_lighting_kernel(
 
         add_in_place(first)
         add_to_pairs(0)
-        warm_bank = new_bank([P, BANK], 6)
+        warm_bank = new_bank([P, BANK], 7)
         for k in range(3):
             nc.tensor.matmul_mx(
                 warm_bank[:], lhsT=w2c[:, 0 : 2 * P].bitcast(FP4X4), lhsT_scale=w2s[:, 0:P],
                 rhs=g2w[:, 0:BANK].bitcast(FP8X4), rhs_scale=g2s[:, 0:BANK], start=True, stop=True,
             )
+        nc.scalar.copy(zb[0][:, 0:half, :], pairs[0][:].rearrange("p u m -> p m u"))
+        nc.vector.tensor_tensor(fourth(0)[:, half:], hist_ps[0, half], last[:, half:BANK], ADD)
         add_to_pairs(1)
         add_to_pairs(2)
-        tail_bank = new_bank([P, 2, P], 4)
-        turn_both(second, (BLOCKS - 1,), tail_bank)
-        for i, (c, lo, hi) in enumerate(pieces):
-            nc.scalar.copy(zb[c][:, lo:hi, :], pairs[i][:].rearrange("p u m -> p m u"))
+        nc.scalar.copy(late[:, 0:half, :], pairs[1][:].rearrange("p u m -> p m u"))
+        nc.scalar.copy(late[:, half : BANK + lead, :], pairs[2][:].rearrange("p u m -> p m u"))
         for c in (0, first, 1):
-            quantise(c)
-        read_out(0, 0, 0)
-        weave(second, (BLOCKS - 1,), tail_bank)
+            quantise(c, c)
         add_in_place(second)
-        read_out(1, 0, 1)
-        read_out(2, first, 0)
-        read_out(3, first, 1)
-        quantise(second)
-        for turn, (c, n) in enumerate(((1, 0), (1, 1), (second, 0), (second, 1)), 4):
-            read_out(turn, c, n)
+        order = [(c, n) for c in (0, first, 1, second) for n in range(N // P)]
+        sums = [multiply(turn, *order[turn]) for turn in range(4)]
+        for turn in range(2 * CHUNKS):
+            if turn == 3:
+                quantise(second, second)
+            read_out(turn, *order[turn], sums[turn])
+            if turn < 2:
+                sums.append(multiply(turn + 4, *order[turn + 4]))
+            if turn == 3:
+                sums.extend(multiply(k, *order[k]) for k in (6, 7))

@@ -146,11 +146,10 @@ def tile_list_woven_probe_lighting_kernel(
         tints.append(load_tint(3))
         wg2_sb = [wg2_pairs, wg2_pairs, load_wg(wg2, 2, "wg2_2")]
         o3 = load_list(offs3, "o3")
-        wg1_third = load_wg(wg1, 2, "wg1_2")
         wg1_pairs = load_wg(wg1, 0, "wg1_pairs")
-        wg1_sb = [wg1_pairs, wg1_pairs, wg1_third]
+        wg1_sb = [wg1_pairs, wg1_pairs, load_wg(wg1, 2, "wg1_2")]
         hist_sb = {}
-        for t, tag in ((2, "hist2"), (0, "tab2w"), (3, "tabw0")):
+        for t, tag in ((0, "tab2w"), (3, "tabw0"), (2, "hist2")):
             hist_sb[t] = load_rows(hist, t, new_tile([P, T2], F32, f"hist{t}", tag))
         wbw = load_words(wb_words[0], "wbw")
         wbs = load_plane(wb_scales[0], "wbs")
@@ -223,7 +222,7 @@ def tile_list_woven_probe_lighting_kernel(
         glossy(2)
         scatter(2, o4, h2, wg2_sb)
 
-        for t in (2, 0, 1, 3):
+        for t in (0, 2, 1, 3):
             for b in range(2):
                 cols = slice(BANK * b, BANK * (b + 1))
                 acc = new_bank([P, BANK], (2 * t + b) % 4)
@@ -243,7 +242,7 @@ def tile_list_woven_probe_lighting_kernel(
         warm = new_tile([P, 1], F32, "warm")
         nc.scalar.activation(warm[:], h2[PACK - 1][:, S - 1 : S], ACT.Sigmoid)
 
-        for t in (2, 0, 1):
+        for t in (0, 2, 1):
             scatter(t, o3, h1, wg1_sb)
         scatter(PACK - 1, o4, h2, wg2_sb)
         wab = new_tile([P, N, PACK], BF16, "wab")
@@ -264,18 +263,21 @@ def tile_list_woven_probe_lighting_kernel(
         def block(c, blk):
             return slice(BANK * c + P * blk, BANK * c + P * (blk + 1))
 
-        def turned_sum(t, c):
-            bank = next_bank([P, BLOCKS, P])
-            for blk in range(BLOCKS):
-                nc.tensor.matmul(bank[:, blk, :], lhsT=hist_sb[t][:, block(c, blk)], rhs=ident[:], is_transpose=True, start=True, stop=False)
-                nc.tensor.matmul(bank[:, blk, :], lhsT=page[t][:, block(c, blk)], rhs=ident[:], is_transpose=True, start=False, stop=True)
-            return bank
+        def turned_sums(t, round_off):
+            held = [new_bank([P, BLOCKS, P], c) for c in range(CHUNKS)]
+            for c in range(CHUNKS):
+                for blk in range(BLOCKS):
+                    nc.tensor.matmul(held[c][:, blk, :], lhsT=hist_sb[t][:, block(c, blk)], rhs=ident[:], is_transpose=True, start=(blk == 0), stop=False)
+            for c in range(CHUNKS):
+                for blk in range(BLOCKS):
+                    nc.tensor.matmul(held[c][:, blk, :], lhsT=page[t][:, block(c, blk)], rhs=ident[:], is_transpose=True, start=False, stop=(blk == BLOCKS - 1))
+                round_off(t, c, held[c])
 
         def words(zt, blk):
             return zt[:].rearrange("m b p e -> m (b p e)").bitcast(F32)[:, P * blk : P * (blk + 1)]
 
         half = BANK // 2
-        lead = 16
+        lead, share, period = 32, 16, 64
         pieces = ((0, 0, half), (1, 0, half), (1, half, BANK))
         pairs = [new_tile([P, 2, half + (lead if i == 2 else 0)], F32, f"pairs{i}") for i in range(len(pieces))]
 
@@ -288,16 +290,6 @@ def tile_list_woven_probe_lighting_kernel(
                 if chunk == c:
                     nc.scalar.copy(pairs[i][:, u, 0:half], bank[:, lo:hi])
 
-        high = [new_tile([P, BLOCKS, P, 2], BF16, f"high{c}") for c in range(CHUNKS)]
-        for c in range(CHUNKS):
-            bank = turned_sum(2, c)
-            nc.scalar.copy(
-                high[c][:].rearrange("m b (g q) e -> m b g q e", g=4),
-                bank[:].rearrange("m b (q g) -> m b g q", g=4).unsqueeze(4).to_broadcast([P, BLOCKS, 4, QUAD, 2]),
-            )
-        for c in on_vector:
-            turn_back(high[c], 1, c, next_bank([P, BANK]))
-
         low = [new_tile([P, BLOCKS, P, 2], BF16, f"low{c}") for c in range(CHUNKS)]
 
         def round_pairs(t, c, bank):
@@ -306,27 +298,32 @@ def tile_list_woven_probe_lighting_kernel(
                 bank[:].rearrange("m b (q g e) -> m b g q e", g=2, e=2),
             )
 
-        for c in range(CHUNKS):
-            round_pairs(0, c, turned_sum(0, c))
-        hist_t = new_tile([P, len(on_vector), BANK], F32, "hist_t", "w1raw0")
-        for c in on_vector:
+        high_all = new_tile([P, CHUNKS, BLOCKS, P, 2], BF16, "high", "w1raw1")
+        nc.gpsimd.memset(high_all[:].rearrange("m c b p e -> m (c b p e)").bitcast(I32), 0)
+        high = [high_all[:, c] for c in range(CHUNKS)]
+
+        def round_singles(t, c, bank):
+            nc.scalar.copy(
+                high[c][:, :, :, 0].rearrange("m b (g q) -> m b g q", g=4),
+                bank[:].rearrange("m b (q g) -> m b g q", g=4),
+            )
+
+        hist_t = new_tile([P, CHUNKS, BANK], F32, "hist_t", "w1raw0")
+        for c in (*on_vector, second):
             bank = next_bank([P, BLOCKS, P])
             for blk in range(BLOCKS):
                 nc.tensor.transpose(bank[:, blk, :], hist_sb[PACK - 1][:, block(c, blk)], ident[:])
             nc.scalar.copy(hist_t[:, c, :], bank[:].rearrange("m b p -> m (b p)"))
-        held = [new_bank([P, BLOCKS, P], c) for c in range(CHUNKS)]
-        for c in range(CHUNKS):
-            for blk in range(BLOCKS):
-                nc.tensor.matmul(held[c][:, blk, :], lhsT=hist_sb[1][:, block(c, blk)], rhs=ident[:], is_transpose=True, start=(blk == 0), stop=False)
-        for c in range(CHUNKS):
-            for blk in range(BLOCKS):
-                nc.tensor.matmul(held[c][:, blk, :], lhsT=page[1][:, block(c, blk)], rhs=ident[:], is_transpose=True, start=False, stop=(blk == BLOCKS - 1))
-            round_pairs(1, c, held[c])
+        turned_sums(0, round_pairs)
+        turned_sums(2, round_singles)
+        for c in on_vector:
+            turn_back(high[c], 1, c, next_bank([P, BANK]))
+        turned_sums(1, round_pairs)
         for c in on_vector:
             turn_back(low[c], 0, c, new_bank([P, BANK], 4 + c))
 
         late = new_tile([P, 2 * BANK, 2], F32, "late", "hist2")
-        zb = [new_tile([P, BANK, 2], F32, "zb0", "w1raw1")[:], late[:, 0:BANK, :], new_tile([P, BANK, 2], F32, "zb2", "tab2w")[:], late[:, BANK:, :]]
+        zb = [new_tile([P, BANK, 2], F32, "zb0")[:], late[:, 0:BANK, :], new_tile([P, BANK, 2], F32, "zb2", "tab2w")[:], late[:, BANK:, :]]
 
         for c, lo, index in ((0, half, 6), (second, 0, 7), (second, half, 0), (first, 0, 1), (first, half, 2)):
             bank = new_bank([P, 2, half], index)
@@ -338,12 +335,13 @@ def tile_list_woven_probe_lighting_kernel(
                 nc.scalar.copy(pairs[2][:, :, half:], bank[:, :, 0:skip])
             nc.scalar.copy(zb[c][:, lo + skip : lo + half, :], bank[:, :, skip:].rearrange("p u m -> p m u"))
         hist_ps = {}
-        for c, lo, hi, index in ((0, 0, half, 7), (0, half, BANK, 0), (1, 0, BANK, 1)):
+        for c, lo, hi, index in ((0, 0, half, 7), (0, half, BANK, 0), (1, 0, BANK, 1), (second, 0, BANK, 2)):
             bank = new_bank([P, hi - lo], index)
             for at in range(lo, hi, P):
                 nc.tensor.transpose(bank[:, at - lo : at - lo + P], hist_t[:, c, at : at + P], ident[:])
             for at in range(lo, hi, half):
                 hist_ps[c, at] = bank[:, at - lo : at - lo + half]
+        hist_last = bank
 
         z = {}
         free_tags = ["h2_0", "h2_1", "linear", "w1b", "h1_0", "h1_1", "h1_2", "h1_3"]
@@ -371,7 +369,7 @@ def tile_list_woven_probe_lighting_kernel(
         def multiply(turn, c, n):
             rows = slice(P * n, P * (n + 1))
             sums = []
-            for wc, ws, banks in ((wbw, wbs, (2, 3, 4, 5)), (wac, was, (6, 0, 1, 7))):
+            for wc, ws, banks in ((wbw, wbs, (3, 4, 5, 2)), (wac, was, (6, 0, 1, 7))):
                 acc = new_bank([P, BANK], banks[turn % 4])
                 nc.tensor.matmul_mx(
                     acc[:], lhsT=wc[:, rows].bitcast(FP8X4), lhsT_scale=ws[:, rows],
@@ -382,7 +380,7 @@ def tile_list_woven_probe_lighting_kernel(
 
         def read_out(turn, c, n, sums):
             rows = slice(P * n, P * (n + 1))
-            gate = new_tile([P, BANK], F32, f"gate{turn}", f"zc{second}" if turn == 1 else None)
+            gate = new_tile([P, BANK], F32, f"gate{turn}", f"zc{second}" if turn == 0 else None)
             nc.scalar.activation(gate[:], sums[0][:], ACT.Sigmoid)
             res = new_tile([P, BANK], F32, "res", free_tags[turn])
             width = BANK // 2 if turn == 2 * CHUNKS - 1 else BANK
@@ -407,7 +405,12 @@ def tile_list_woven_probe_lighting_kernel(
         nc.scalar.copy(late[:, half : BANK + lead, :], pairs[2][:].rearrange("p u m -> p m u"))
         for c in (0, first, 1):
             quantise(c, c)
-        add_in_place(second)
+        runs = [
+            ap.rearrange("p (r m) -> p r m", m=period)
+            for ap in (fourth(second), last[:, BANK * second :], hist_last[:], hist_sb[PACK - 1][:, BANK * second :])
+        ]
+        nc.vector.tensor_tensor(runs[0][:, :, 0:share], runs[2][:, :, 0:share], runs[1][:, :, 0:share], ADD)
+        nc.gpsimd.tensor_tensor(runs[0][:, :, share:], runs[1][:, :, share:], runs[3][:, :, share:], ADD)
         order = [(c, n) for c in (0, first, 1, second) for n in range(N // P)]
         sums = [multiply(turn, *order[turn]) for turn in range(4)]
         for turn in range(2 * CHUNKS):

@@ -53,13 +53,6 @@ def tile_list_woven_probe_lighting_kernel(
             nc.sync.dma_start(dst[:].bitcast(I32), src.rearrange("p n i -> p (n i)").bitcast(I32))
             return dst
 
-        def load_repeated(rows, name):
-            count, cols = rows.shape
-            dst = new_tile([P, cols], U8, name)
-            words = rows.bitcast(I32).unsqueeze(1).to_broadcast([count, P // count, cols // 4])
-            nc.sync.dma_start(dst[:].bitcast(I32), words)
-            return dst
-
         def new_plane(cols, name):
             dst = new_tile([P, cols], U8, name)
             nc.gpsimd.memset(dst[:].bitcast(I32), 0)
@@ -101,7 +94,10 @@ def tile_list_woven_probe_lighting_kernel(
             return load_rows(tint_col, page, new_tile([P, 1], F32, f"tint{page}"))
 
         o1 = load_list(offs, "o1")
-        tabs = load_repeated(tab_scales.rearrange("a q t -> (a q) t"), "tabs")
+        tabs = new_tile([P, T], U8, "tabs")
+        nc.sync.dma_start(tabs[0:QUAD, :].bitcast(I32), tab_scales.rearrange("a q t -> (a q) t").bitcast(I32))
+        nc.vector.memset(tabs[QUAD : 2 * QUAD, :].bitcast(I32), 0)
+        nc.vector.memset(tabs[2 * QUAD :, :].bitcast(I32), 0)
         o2 = load_list(offs2, "o2")
         tab2s = new_tile([P, T], U8, "tab2s")
         for q in range(4):
@@ -140,14 +136,14 @@ def tile_list_woven_probe_lighting_kernel(
             for r in range(4):
                 nc.sync.dma_start(
                     g1s[4 * a + r : P : QUAD, :].bitcast(I32),
-                    g1rows[64 * a + 4 * r : 64 * (a + 1) : 16, :].bitcast(I32),
+                    g1rows[16 * a + r : 16 * (a + 1) : 4, :].bitcast(I32),
                 )
 
         tints.append(load_tint(3))
         wg2_sb = [wg2_pairs, wg2_pairs, load_wg(wg2, 2, "wg2_2")]
-        o3 = load_list(offs3, "o3")
         wg1_pairs = load_wg(wg1, 0, "wg1_pairs")
         wg1_sb = [wg1_pairs, wg1_pairs, load_wg(wg1, 2, "wg1_2")]
+        o3 = load_list(offs3, "o3")
         hist_sb = {}
         for t, tag in ((0, "tab2w"), (3, "tabw0"), (2, "hist2")):
             hist_sb[t] = load_rows(hist, t, new_tile([P, T2], F32, f"hist{t}", tag))

@@ -150,10 +150,12 @@ def tile_list_woven_probe_lighting_kernel(
         wbw = load_words(wb_words[0], "wbw")
         wbs = load_plane(wb_scales[0], "wbs")
         wg2_sb.append(load_wg(wg2, 3, "wg2_3"))
-        waraw = new_tile([P, PACK, N], F32, "waraw")
-        nc.sync.dma_start(waraw[:], wa.rearrange("(p j) c -> p j c", j=PACK))
+        waraw = [new_tile([P, PACK, P], F32, f"waraw{n}") for n in range(2)]
+        wa_rows = wa.rearrange("(p j) c -> p j c", j=PACK)
+        nc.sync.dma_start(waraw[0][:], wa_rows[:, :, 0:P])
         hist_sb[1] = load_rows(hist, 1, new_tile([P, T2], F32, "hist1", "tabw1"))
         wg1_sb.append(load_wg(wg1, 3, "wg1_3"))
+        nc.sync.dma_start(waraw[1][:], wa_rows[:, :, P:])
 
         w2c = new_tile([P, 2 * H], U8, "w2c")
         w2s = new_tile([P, H], U8, "w2s")
@@ -241,12 +243,18 @@ def tile_list_woven_probe_lighting_kernel(
         for t in (0, 2, 1):
             scatter(t, o3, h1, wg1_sb)
         scatter(PACK - 1, o4, h2, wg2_sb)
-        wab = new_tile([P, N, PACK], BF16, "wab")
-        nc.scalar.copy(wab[:], waraw[:].rearrange("p j n -> p n j"))
         wac = new_tile([P, N], U32, "wac")
         was = new_tile([P, N], U8, "was")
-        nc.vector.quantize_mx(wac[:].bitcast(FP8X4), was[:], wab[:].rearrange("p n j -> p (n j)"))
+
+        def quantise_wa(n):
+            wab = new_tile([P, P, PACK], BF16, f"wab{n}")
+            nc.scalar.copy(wab[:], waraw[n][:].rearrange("p j n -> p n j"))
+            rows = slice(P * n, P * (n + 1))
+            nc.vector.quantize_mx(wac[:, rows].bitcast(FP8X4), was[:, rows], wab[:].rearrange("p n j -> p (n j)"))
+
+        quantise_wa(0)
         scatter(PACK - 1, o3, h1, wg1_sb)
+        quantise_wa(1)
 
         on_vector = (0, 1)
         first, second = 2, 3
@@ -273,7 +281,7 @@ def tile_list_woven_probe_lighting_kernel(
             return zt[:].rearrange("m b p e -> m (b p e)").bitcast(F32)[:, P * blk : P * (blk + 1)]
 
         half = BANK // 2
-        lead, share, period = 32, 16, 64
+        lead = 32
         pieces = ((0, 0, half), (1, 0, half), (1, half, BANK))
         pairs = [new_tile([P, 2, half + (lead if i == 2 else 0)], F32, f"pairs{i}") for i in range(len(pieces))]
 
@@ -305,7 +313,7 @@ def tile_list_woven_probe_lighting_kernel(
             )
 
         hist_t = new_tile([P, CHUNKS, BANK], F32, "hist_t", "w1raw0")
-        for c in (*on_vector, second):
+        for c in on_vector:
             bank = next_bank([P, BLOCKS, P])
             for blk in range(BLOCKS):
                 nc.tensor.transpose(bank[:, blk, :], hist_sb[PACK - 1][:, block(c, blk)], ident[:])
@@ -331,17 +339,16 @@ def tile_list_woven_probe_lighting_kernel(
                 nc.scalar.copy(pairs[2][:, :, half:], bank[:, :, 0:skip])
             nc.scalar.copy(zb[c][:, lo + skip : lo + half, :], bank[:, :, skip:].rearrange("p u m -> p m u"))
         hist_ps = {}
-        for c, lo, hi, index in ((0, 0, half, 7), (0, half, BANK, 0), (1, 0, BANK, 1), (second, 0, BANK, 2)):
+        for c, lo, hi, index in ((0, 0, half, 7), (1, 0, BANK, 0), (0, half, BANK, 1)):
             bank = new_bank([P, hi - lo], index)
             for at in range(lo, hi, P):
                 nc.tensor.transpose(bank[:, at - lo : at - lo + P], hist_t[:, c, at : at + P], ident[:])
             for at in range(lo, hi, half):
                 hist_ps[c, at] = bank[:, at - lo : at - lo + half]
-        hist_last = bank
 
-        z = {}
-        free_tags = ["h2_0", "h2_1", "linear", "w1b", "h1_0", "h1_1", "h1_2", "h1_3"]
+        free_tags = ["h2_0", "h2_1", "linear", "wg1_pairs", "h1_0", "h1_1", "h1_2", "h1_3"]
         last = page[PACK - 1]
+        by_half = out.rearrange("(n p) m -> p n m", n=2)
 
         def rounded(c):
             return zb[c].rearrange("p m u -> p (m u)").bitcast(BF16)
@@ -358,33 +365,44 @@ def tile_list_woven_probe_lighting_kernel(
             halves = pairs[i][:, 1, 0:half].bitcast(BF16).rearrange("p (m e) -> p m e", e=2)
             nc.vector.tensor_tensor(halves[:, :, 1], hist_ps[c, lo], last[:, BANK * c + lo : BANK * c + hi], ADD)
 
-        def quantise(c, tag):
-            z[c] = (new_tile([P, BANK], U32, f"zc{c}", f"zc{tag}"), new_tile([P, BANK], U8, f"zs{c}"))
-            nc.vector.quantize_mx(z[c][0][:].bitcast(FP8X4), z[c][1][:], rounded(c))
+        def quantise(c, lo, hi, tag=None):
+            codes = new_tile([P, hi - lo], U32, f"zc{c}_{lo}", tag)
+            scales = new_tile([P, hi - lo], U8, f"zs{c}_{lo}")
+            nc.vector.quantize_mx(codes[:].bitcast(FP8X4), scales[:], rounded(c)[:, PACK * lo : PACK * hi])
+            return codes, scales
 
-        def multiply(turn, c, n):
-            rows = slice(P * n, P * (n + 1))
-            sums = []
-            for wc, ws, banks in ((wbw, wbs, (3, 4, 5, 2)), (wac, was, (6, 0, 1, 7))):
-                acc = new_bank([P, BANK], banks[turn % 4])
+        def passes(weights, index, z, halves):
+            width = z[0].shape[1]
+            acc = new_bank([P, len(halves), width], index)
+            for i, n in enumerate(halves):
+                rows = slice(P * n, P * (n + 1))
                 nc.tensor.matmul_mx(
-                    acc[:], lhsT=wc[:, rows].bitcast(FP8X4), lhsT_scale=ws[:, rows],
-                    rhs=z[c][0][:].bitcast(FP8X4), rhs_scale=z[c][1][:], start=True, stop=True,
+                    acc[:, i, :], lhsT=weights[0][:, rows].bitcast(FP8X4), lhsT_scale=weights[1][:, rows],
+                    rhs=z[0][:].bitcast(FP8X4), rhs_scale=z[1][:], start=True, stop=True,
                 )
-                sums.append(acc)
-            return sums
+            return acc
 
-        def read_out(turn, c, n, sums):
-            rows = slice(P * n, P * (n + 1))
-            gate = new_tile([P, BANK], F32, f"gate{turn}", f"zc{second}" if turn == 0 else None)
-            nc.scalar.activation(gate[:], sums[0][:], ACT.Sigmoid)
-            res = new_tile([P, BANK], F32, "res", free_tags[turn])
-            width = BANK // 2 if turn == 2 * CHUNKS - 1 else BANK
-            for lo in range(0, BANK, width):
-                part = slice(lo, lo + width)
-                nc.vector.tensor_tensor(res[:, part], sums[1][:, part], gate[:, part], MULT)
-                nc.sync.dma_start(out[rows, BANK * c + lo : BANK * c + lo + width], res[:, part])
+        vis_banks = (3, 4, 5, 2)
+        light_banks = (6, 0, 1, 7)
+        gate_tags = {1: "late_a", 2: "late_b"}
 
+        def multiply(turn, z, halves, parts):
+            vis = passes((wbw, wbs), vis_banks[turn % 4], z, halves)
+            light = passes((wac, was), light_banks[turn % 4], z, halves)
+            gate = new_tile(list(vis.shape), F32, f"gate{turn}", gate_tags.get(turn))
+            for part in parts:
+                nc.scalar.activation(gate[:, part, :], vis[:, part, :], ACT.Sigmoid)
+            return light, gate
+
+        def read_out(turn, at, halves, parts, light, gate):
+            res = new_tile(list(light.shape), F32, f"res{turn}", free_tags[turn])
+            width = light.shape[2]
+            dst = by_half[:, halves[0] : halves[-1] + 1, at : at + width]
+            for part in parts:
+                nc.vector.tensor_tensor(res[:, part, :], light[:, part, :], gate[:, part, :], MULT)
+                nc.sync.dma_start(dst[:, part, :], res[:, part, :])
+
+        both, whole, apart, one = (0, 1), (slice(0, 2),), (slice(0, 1), slice(1, 2)), (slice(0, 1),)
         add_in_place(first)
         add_to_pairs(0)
         warm_bank = new_bank([P, BANK], 7)
@@ -394,26 +412,25 @@ def tile_list_woven_probe_lighting_kernel(
                 rhs=g2w[:, 0:BANK].bitcast(FP8X4), rhs_scale=g2s[:, 0:BANK], start=True, stop=True,
             )
         nc.scalar.copy(zb[0][:, 0:half, :], pairs[0][:].rearrange("p u m -> p m u"))
-        nc.vector.tensor_tensor(fourth(0)[:, half:], hist_ps[0, half], last[:, half:BANK], ADD)
         add_to_pairs(1)
         add_to_pairs(2)
+        nc.vector.tensor_tensor(fourth(0)[:, half:], hist_ps[0, half], last[:, half:BANK], ADD)
         nc.scalar.copy(late[:, 0:half, :], pairs[1][:].rearrange("p u m -> p m u"))
         nc.scalar.copy(late[:, half : BANK + lead, :], pairs[2][:].rearrange("p u m -> p m u"))
-        for c in (0, first, 1):
-            quantise(c, c)
-        runs = [
-            ap.rearrange("p (r m) -> p r m", m=period)
-            for ap in (fourth(second), last[:, BANK * second :], hist_last[:], hist_sb[PACK - 1][:, BANK * second :])
+        z = [quantise(0, 0, half), quantise(0, half, BANK), quantise(first, 0, BANK), quantise(1, 0, BANK)]
+        add_in_place(second)
+        turns = [
+            (z[0], 0, both, apart, whole), (z[1], half, both, whole, whole),
+            (z[2], BANK * first, (0,), one, one), (z[2], BANK * first, (1,), one, one),
+            (z[3], BANK, (0,), one, one), (z[3], BANK, (1,), one, one),
         ]
-        nc.vector.tensor_tensor(runs[0][:, :, 0:share], runs[2][:, :, 0:share], runs[1][:, :, 0:share], ADD)
-        nc.gpsimd.tensor_tensor(runs[0][:, :, share:], runs[1][:, :, share:], runs[3][:, :, share:], ADD)
-        order = [(c, n) for c in (0, first, 1, second) for n in range(N // P)]
-        sums = [multiply(turn, *order[turn]) for turn in range(4)]
-        for turn in range(2 * CHUNKS):
-            if turn == 3:
-                quantise(second, second)
-            read_out(turn, *order[turn], sums[turn])
+        ready = [multiply(turn, turns[turn][0], turns[turn][2], turns[turn][3]) for turn in range(4)]
+        for turn in range(4):
+            read_out(turn, turns[turn][1], turns[turn][2], turns[turn][4], *ready[turn])
             if turn < 2:
-                sums.append(multiply(turn + 4, *order[turn + 4]))
-            if turn == 3:
-                sums.extend(multiply(k, *order[k]) for k in (6, 7))
+                ready.append(multiply(turn + 4, turns[turn + 4][0], turns[turn + 4][2], turns[turn + 4][3]))
+        for lo, tag in ((0, "late_a"), (half, "late_b")):
+            turns.append((quantise(second, lo, lo + half, tag), BANK * second + lo, both, whole, apart if lo else whole))
+        ready.extend(multiply(turn, turns[turn][0], turns[turn][2], turns[turn][3]) for turn in (6, 7))
+        for turn in range(4, 8):
+            read_out(turn, turns[turn][1], turns[turn][2], turns[turn][4], *ready[turn])

@@ -109,9 +109,10 @@ def tile_list_woven_probe_lighting_kernel(
         w2raw = new_tile([P, 2 * H], U8, "w2raw")
         nc.sync.dma_start(w2raw[:].bitcast(I32), w2_words[0].bitcast(I32))
         w2sraw = load_plane(w2_scales[0], "w2sraw")
-        tabw = [load_words(tab_words[a], f"tabw{a}") for a in range(2)]
-        wg2_pairs = load_wg(wg2, 0, "wg2_pairs")
+        tabw = [load_words(tab_words[0], "tabw0")]
         tints = [load_tint(0)]
+        tabw.append(load_words(tab_words[1], "tabw1"))
+        wg2_pairs = load_wg(wg2, 0, "wg2_pairs")
         o4 = load_list(offs4, "o4")
         w1raw = []
         for a in range(2):

@@ -257,8 +257,8 @@ def tile_list_woven_probe_lighting_kernel(
         scatter(PACK - 1, o3, h1, wg1_sb)
         quantise_wa(1)
 
-        on_vector = (0, 1)
-        first, second = 2, 3
+        on_vector = (0, 2)
+        first, mid, second = 1, 2, 3
         ring = [0]
 
         def next_bank(shape):
@@ -283,7 +283,8 @@ def tile_list_woven_probe_lighting_kernel(
 
         half = BANK // 2
         lead = 32
-        pieces = ((0, 0, half), (1, 0, half), (1, half, BANK))
+        give = 48
+        pieces = ((0, 0, half), (mid, 0, half), (mid, half, BANK))
         pairs = [new_tile([P, 2, half + (lead if i == 2 else 0)], F32, f"pairs{i}") for i in range(len(pieces))]
 
         def turn_back(zt, u, c, bank):
@@ -325,10 +326,11 @@ def tile_list_woven_probe_lighting_kernel(
             turn_back(high[c], 1, c, next_bank([P, BANK]))
         turned_sums(1, round_pairs)
         for c in on_vector:
-            turn_back(low[c], 0, c, new_bank([P, BANK], 4 + c))
+            turn_back(low[c], 0, c, new_bank([P, BANK], 4 + c // 2))
 
         late = new_tile([P, 2 * BANK, 2], F32, "late", "hist2")
-        zb = [new_tile([P, BANK, 2], F32, "zb0")[:], late[:, 0:BANK, :], new_tile([P, BANK, 2], F32, "zb2", "tab2w")[:], late[:, BANK:, :]]
+        early = new_tile([P, 2 * BANK, 2], F32, "early", "tab2w")
+        zb = [early[:, 0:BANK, :], early[:, BANK:, :], late[:, 0:BANK, :], late[:, BANK:, :]]
 
         for c, lo, index in ((0, half, 6), (second, 0, 7), (second, half, 0), (first, 0, 1), (first, half, 2)):
             bank = new_bank([P, 2, half], index)
@@ -340,12 +342,11 @@ def tile_list_woven_probe_lighting_kernel(
                 nc.scalar.copy(pairs[2][:, :, half:], bank[:, :, 0:skip])
             nc.scalar.copy(zb[c][:, lo + skip : lo + half, :], bank[:, :, skip:].rearrange("p u m -> p m u"))
         hist_ps = {}
-        for c, lo, hi, index in ((0, 0, half, 7), (1, 0, BANK, 0), (0, half, BANK, 1)):
+        for c, lo, hi, index in ((0, 0, P, 6), (0, P, half, 7), (mid, 0, BANK, 0), (0, half, BANK, 1)):
             bank = new_bank([P, hi - lo], index)
             for at in range(lo, hi, P):
                 nc.tensor.transpose(bank[:, at - lo : at - lo + P], hist_t[:, c, at : at + P], ident[:])
-            for at in range(lo, hi, half):
-                hist_ps[c, at] = bank[:, at - lo : at - lo + half]
+            hist_ps[c, lo] = bank
 
         free_tags = ["h2_0", "h2_1", "linear", "wg1_pairs", "h1_0", "h1_1", "h1_2", "h1_3"]
         last = page[PACK - 1]
@@ -357,14 +358,14 @@ def tile_list_woven_probe_lighting_kernel(
         def fourth(c):
             return rounded(c).rearrange("p (m j) -> p m j", j=PACK)[:, :, PACK - 1]
 
-        def add_in_place(c):
-            cols = slice(BANK * c, BANK * (c + 1))
-            nc.gpsimd.tensor_tensor(fourth(c), last[:, cols], hist_sb[PACK - 1][:, cols], ADD)
+        def add_in_place(tile, base, lo, hi):
+            dst = tile[:, lo - base : hi - base, :].rearrange("p m u -> p (m u)").bitcast(BF16).rearrange("p (m j) -> p m j", j=PACK)
+            nc.gpsimd.tensor_tensor(dst[:, :, PACK - 1], last[:, lo:hi], hist_sb[PACK - 1][:, lo:hi], ADD)
 
-        def add_to_pairs(i):
-            c, lo, hi = pieces[i]
-            halves = pairs[i][:, 1, 0:half].bitcast(BF16).rearrange("p (m e) -> p m e", e=2)
-            nc.vector.tensor_tensor(halves[:, :, 1], hist_ps[c, lo], last[:, BANK * c + lo : BANK * c + hi], ADD)
+        def add_to_pairs(i, lo, hi, held):
+            c, base = pieces[i][0:2]
+            halves = pairs[i][:, 1, lo - base : hi - base].bitcast(BF16).rearrange("p (m e) -> p m e", e=2)
+            nc.vector.tensor_tensor(halves[:, :, 1], held, last[:, BANK * c + lo : BANK * c + hi], ADD)
 
         def quantise(c, lo, hi, tag=None):
             codes = new_tile([P, hi - lo], U32, f"zc{c}_{lo}", tag)
@@ -388,11 +389,11 @@ def tile_list_woven_probe_lighting_kernel(
         gate_tags = {1: "late_a", 2: "late_b"}
 
         def multiply(turn, z, halves, parts):
-            vis = passes((wbw, wbs), vis_banks[turn % 4], z, halves)
+            vis = [passes((wbw, wbs), vis_banks[(turn - i) % 4], z, halves[part]) for i, part in enumerate(parts)]
             light = passes((wac, was), light_banks[turn % 4], z, halves)
-            gate = new_tile(list(vis.shape), F32, f"gate{turn}", gate_tags.get(turn))
-            for part in parts:
-                nc.scalar.activation(gate[:, part, :], vis[:, part, :], ACT.Sigmoid)
+            gate = new_tile(list(light.shape), F32, f"gate{turn}", gate_tags.get(turn))
+            for acc, part in zip(vis, parts):
+                nc.scalar.activation(gate[:, part, :], acc[:], ACT.Sigmoid)
             return light, gate
 
         def read_out(turn, at, halves, parts, light, gate):
@@ -404,26 +405,27 @@ def tile_list_woven_probe_lighting_kernel(
                 nc.sync.dma_start(dst[:, part, :], res[:, part, :])
 
         both, whole, apart, one = (0, 1), (slice(0, 2),), (slice(0, 1), slice(1, 2)), (slice(0, 1),)
-        add_in_place(first)
-        add_to_pairs(0)
-        warm_bank = new_bank([P, BANK], 7)
+        add_in_place(early, 0, BANK - give, 2 * BANK)
+        add_to_pairs(0, 0, P, hist_ps[0, 0][:])
+        add_to_pairs(0, P, half, hist_ps[0, P][:])
+        warm_bank = new_bank([P, BANK], 6)
         for k in range(3):
             nc.tensor.matmul_mx(
                 warm_bank[:], lhsT=w2c[:, 0 : 2 * P].bitcast(FP4X4), lhsT_scale=w2s[:, 0:P],
                 rhs=g2w[:, 0:BANK].bitcast(FP8X4), rhs_scale=g2s[:, 0:BANK], start=True, stop=True,
             )
         nc.scalar.copy(zb[0][:, 0:half, :], pairs[0][:].rearrange("p u m -> p m u"))
-        add_to_pairs(1)
-        add_to_pairs(2)
-        nc.vector.tensor_tensor(fourth(0)[:, half:], hist_ps[0, half], last[:, half:BANK], ADD)
+        add_to_pairs(1, 0, half, hist_ps[mid, 0][:, 0:half])
+        add_to_pairs(2, half, BANK, hist_ps[mid, 0][:, half:])
+        nc.vector.tensor_tensor(fourth(0)[:, half : BANK - give], hist_ps[0, half][:, 0 : half - give], last[:, half : BANK - give], ADD)
         nc.scalar.copy(late[:, 0:half, :], pairs[1][:].rearrange("p u m -> p m u"))
         nc.scalar.copy(late[:, half : BANK + lead, :], pairs[2][:].rearrange("p u m -> p m u"))
-        z = [quantise(0, 0, half), quantise(0, half, BANK), quantise(first, 0, BANK), quantise(1, 0, BANK)]
-        add_in_place(second)
+        z = [quantise(0, 0, half), quantise(0, half, BANK), quantise(first, 0, BANK), quantise(mid, 0, BANK)]
+        add_in_place(late, 2 * BANK, 3 * BANK, T2)
         turns = [
             (z[0], 0, both, apart, whole), (z[1], half, both, whole, whole),
             (z[2], BANK * first, (0,), one, one), (z[2], BANK * first, (1,), one, one),
-            (z[3], BANK, (0,), one, one), (z[3], BANK, (1,), one, one),
+            (z[3], BANK * mid, (0,), one, one), (z[3], BANK * mid, (1,), one, one),
         ]
         ready = [multiply(turn, turns[turn][0], turns[turn][2], turns[turn][3]) for turn in range(4)]
         for turn in range(4):

@@ -384,12 +384,12 @@ def tile_list_woven_probe_lighting_kernel(
                 )
             return acc
 
-        vis_banks = (3, 4, 5, 2)
+        vis_banks = ((3, 2), (4,), (5,), (2,), (3,), (4,), (5,), (2, 3))
         light_banks = (6, 0, 1, 7)
         gate_tags = {1: "late_a", 2: "late_b"}
 
         def multiply(turn, z, halves, parts):
-            vis = [passes((wbw, wbs), vis_banks[(turn - i) % 4], z, halves[part]) for i, part in enumerate(parts)]
+            vis = [passes((wbw, wbs), index, z, halves[part]) for index, part in zip(vis_banks[turn], parts)]
             light = passes((wac, was), light_banks[turn % 4], z, halves)
             gate = new_tile(list(light.shape), F32, f"gate{turn}", gate_tags.get(turn))
             for acc, part in zip(vis, parts):
@@ -432,8 +432,10 @@ def tile_list_woven_probe_lighting_kernel(
             read_out(turn, turns[turn][1], turns[turn][2], turns[turn][4], *ready[turn])
             if turn < 2:
                 ready.append(multiply(turn + 4, turns[turn + 4][0], turns[turn + 4][2], turns[turn + 4][3]))
-        for lo, tag in ((0, "late_a"), (half, "late_b")):
-            turns.append((quantise(second, lo, lo + half, tag), BANK * second + lo, both, whole, apart if lo else whole))
-        ready.extend(multiply(turn, turns[turn][0], turns[turn][2], turns[turn][3]) for turn in (6, 7))
         for turn in range(4, 8):
+            if turn < 6:
+                lo = half * (turn - 4)
+                parts = apart if lo else whole
+                turns.append((quantise(second, lo, lo + half, gate_tags[turn - 3]), BANK * second + lo, both, parts, parts))
+                ready.append(multiply(turn + 2, turns[turn + 2][0], both, parts))
             read_out(turn, turns[turn][1], turns[turn][2], turns[turn][4], *ready[turn])

@@ -388,13 +388,16 @@ def tile_list_woven_probe_lighting_kernel(
         light_banks = (6, 0, 1, 7)
         gate_tags = {1: "late_a", 2: "late_b"}
 
-        def multiply(turn, z, halves, parts):
+        def gate_of(turn, z, halves, parts):
             vis = [passes((wbw, wbs), index, z, halves[part]) for index, part in zip(vis_banks[turn], parts)]
-            light = passes((wac, was), light_banks[turn % 4], z, halves)
-            gate = new_tile(list(light.shape), F32, f"gate{turn}", gate_tags.get(turn))
+            gate = new_tile([P, len(halves), z[0].shape[1]], F32, f"gate{turn}", gate_tags.get(turn))
             for acc, part in zip(vis, parts):
                 nc.scalar.activation(gate[:, part, :], acc[:], ACT.Sigmoid)
-            return light, gate
+            return gate
+
+        def multiply(turn, z, halves, parts):
+            gate = gate_of(turn, z, halves, parts)
+            return passes((wac, was), light_banks[turn % 4], z, halves), gate
 
         def read_out(turn, at, halves, parts, light, gate):
             res = new_tile(list(light.shape), F32, f"res{turn}", free_tags[turn])
@@ -427,7 +430,9 @@ def tile_list_woven_probe_lighting_kernel(
             (z[2], BANK * first, (0,), one, one), (z[2], BANK * first, (1,), one, one),
             (z[3], BANK * mid, (0,), one, one), (z[3], BANK * mid, (1,), one, one),
         ]
-        ready = [multiply(turn, turns[turn][0], turns[turn][2], turns[turn][3]) for turn in range(4)]
+        gates = [gate_of(turn, turns[turn][0], turns[turn][2], turns[turn][3]) for turn in range(2)]
+        ready = [(passes((wac, was), light_banks[turn], turns[turn][0], both), gates[turn]) for turn in range(2)]
+        ready.extend(multiply(turn, turns[turn][0], turns[turn][2], turns[turn][3]) for turn in (2, 3))
         for turn in range(4):
             read_out(turn, turns[turn][1], turns[turn][2], turns[turn][4], *ready[turn])
             if turn < 2:

from contextlib import ExitStack

import concourse.mybir as mybir
from concourse.masks import make_identity

K, K2, H, N, T, S, T2 = 1024, 512, 512, 256, 2048, 1024, 2048
FLOPS = 2 * (K * H * S + K2 * H * S + 2 * H * N * T2)

F32 = mybir.dt.float32
BF16 = mybir.dt.bfloat16
I32 = mybir.dt.int32
U32 = mybir.dt.uint32
U16 = mybir.dt.uint16
U8 = mybir.dt.uint8
FP8X4 = mybir.dt.float8_e4m3fn_x4
FP4X4 = mybir.dt.float4_e2m1fn_x4
ACT = mybir.ActivationFunctionType
MULT = mybir.AluOpType.mult
ADD = mybir.AluOpType.add

P = 128
PACK = 4
QUAD = 32
BANK = 512
AL = 64
CHUNKS = T2 // BANK
BLOCKS = BANK // P


def tile_list_woven_probe_lighting_kernel(
    tc, tab_words, tab_scales, tab2_words, tab2_scales, offs, offs2, offs3, offs4,
    w1, w2_words, w2_scales, tint, wg1, wg2, hist, wa, wb_words, wb_scales, out,
):
    nc = tc.nc
    with ExitStack() as ctx:
        lists = ctx.enter_context(tc.tile_pool(name="lists", bufs=1))
        sb = ctx.enter_context(tc.tile_pool(name="sb", bufs=1))
        ps = ctx.enter_context(tc.psum_pool(name="ps", bufs=1))

        def new_tile(shape, dtype, name, tag=None, bufs=1):
            return sb.tile(shape, dtype, name=name, tag=tag or name, bufs=bufs, align_bytes=AL)

        def new_bank(shape, index):
            return ps.tile(shape, F32, name=f"bank{index}", tag=f"bank{index}")

        def load_list(src, name):
            dst = lists.tile([P, S // 16], U16, name=name)
            nc.sync.dma_start(dst[:], src)
            return dst

        def load_words(src, name):
            dst = new_tile([P, src.shape[1]], U32, name)
            nc.sync.dma_start(dst[:].bitcast(I32), src.rearrange("p n i -> p (n i)").bitcast(I32))
            return dst

        def new_plane(cols, name):
            dst = new_tile([P, cols], U8, name)
            nc.gpsimd.memset(dst[:].bitcast(I32), 0)
            return dst

        def load_plane(src, name):
            dst = new_plane(src.shape[1], name)
            for q in range(4):
                nc.sync.dma_start(dst[QUAD * q : QUAD * q + 4, :].bitcast(I32), src[4 * q : 4 * q + 4, :].bitcast(I32))
            return dst

        def load_wg(src, page, name):
            dst = new_tile([P, S], F32, name)
            rows = src.rearrange("(q t) j -> t q j", t=PACK)
            if page == 0:
                for e in range(2):
                    nc.sync.dma_start(dst[e:P:2, :], rows[e].unsqueeze(1).to_broadcast([QUAD, 2, S]))
            elif page == 2:
                nc.sync.dma_start(dst[:], rows[2].unsqueeze(1).to_broadcast([QUAD, 4, S]))
            else:
                for g in (0, 2, 1, 3):
                    nc.sync.dma_start(dst[QUAD * g : QUAD * (g + 1), :], rows[3])
            return dst

        def load_rows(src, page, dst):
            if page < 2:
                rows = src.rearrange("(h g q t) m -> h t q g m", h=2, g=2, t=PACK)[page]
                for e in range(2):
                    nc.sync.dma_start(dst[e:P:2, :], rows[e])
            elif page == 2:
                nc.sync.dma_start(dst[:], src.rearrange("(g q t) m -> t q g m", g=4, t=PACK)[2])
            else:
                nc.sync.dma_start(dst[:], src.rearrange("(p t) m -> t p m", t=PACK)[3])
            return dst

        tint_col = tint.rearrange("(r m) -> r m", m=1)

        def load_tint(page):
            return load_rows(tint_col, page, new_tile([P, 1], F32, f"tint{page}"))

        o1 = load_list(offs, "o1")
        tabs = new_tile([P, T], U8, "tabs")
        nc.sync.dma_start(tabs[0:QUAD, :].bitcast(I32), tab_scales.rearrange("a q t -> (a q) t").bitcast(I32))
        nc.vector.memset(tabs[QUAD : 2 * QUAD, :].bitcast(I32), 0)
        nc.vector.memset(tabs[2 * QUAD :, :].bitcast(I32), 0)
        o2 = load_list(offs2, "o2")
        tab2s = new_tile([P, T], U8, "tab2s")
        for q in range(4):
            nc.sync.dma_start(
                tab2s[QUAD * q : QUAD * (q + 1), :].bitcast(I32),
                tab2_scales[0, 4 * q : 4 * q + 4, :].bitcast(I32).partition_broadcast(QUAD // 4),
            )
        tab2w = load_words(tab2_words[0], "tab2w")
        w2raw = new_tile([P, 2 * H], U8, "w2raw")
        nc.sync.dma_start(w2raw[:].bitcast(I32), w2_words[0].bitcast(I32))
        w2sraw = load_plane(w2_scales[0], "w2sraw")
        tabw = [load_words(tab_words[0], "tabw0")]
        tints = [load_tint(0)]
        tabw.append(load_words(tab_words[1], "tabw1"))
        wg2_pairs = load_wg(wg2, 0, "wg2_pairs")
        o4 = load_list(offs4, "o4")
        w1raw = []
        for a in range(2):
            raw = new_tile([P, PACK, H], F32, f"w1raw{a}")
            nc.sync.dma_start(raw[:], w1[512 * a : 512 * (a + 1), :].rearrange("(p j) c -> p j c", j=PACK))
            w1raw.append(raw)
            tints.append(load_tint(1 + a))
        g1s = new_plane(S, "g1s")
        ident = new_tile([P, P], F32, "ident")
        make_identity(nc, ident[:])

        g1rows = new_tile([P, S], U8, "g1rows")
        nc.vector.tensor_copy(g1rows[:], tabs[:].indirect(o1[:]))
        g2s = new_tile([P, S], U8, "g2s")
        nc.vector.tensor_copy(g2s[:], tab2s[:].indirect(o2[:]))
        g2w = new_tile([P, S], U32, "g2w")
        nc.vector.tensor_copy(g2w[:], tab2w[:].indirect(o2[:]))
        g1w = new_tile([P, 2, S], U32, "g1w")
        for a in range(2):
            nc.vector.tensor_copy(g1w[:, a, :], tabw[a][:].indirect(o1[:]))
        for a in range(2):
            for r in range(4):
                nc.sync.dma_start(
                    g1s[4 * a + r : P : QUAD, :].bitcast(I32),
                    g1rows[16 * a + r : 16 * (a + 1) : 4, :].bitcast(I32),
                )

        tints.append(load_tint(3))
        wg2_sb = [wg2_pairs, wg2_pairs, load_wg(wg2, 2, "wg2_2")]
        wg1_pairs = load_wg(wg1, 0, "wg1_pairs")
        wg1_sb = [wg1_pairs, wg1_pairs, load_wg(wg1, 2, "wg1_2")]
        o3 = load_list(offs3, "o3")
        hist_sb = {}
        for t, tag in ((0, "tab2w"), (3, "tabw0"), (2, "hist2")):
            hist_sb[t] = load_rows(hist, t, new_tile([P, T2], F32, f"hist{t}", tag))
        wbw = load_words(wb_words[0], "wbw")
        wbs = load_plane(wb_scales[0], "wbs")
        wg2_sb.append(load_wg(wg2, 3, "wg2_3"))
        waraw = [new_tile([P, PACK, P], F32, f"waraw{n}") for n in range(2)]
        wa_rows = wa.rearrange("(p j) c -> p j c", j=PACK)
        nc.sync.dma_start(waraw[0][:], wa_rows[:, :, 0:P])
        hist_sb[1] = load_rows(hist, 1, new_tile([P, T2], F32, "hist1", "tabw1"))
        wg1_sb.append(load_wg(wg1, 3, "wg1_3"))
        nc.sync.dma_start(waraw[1][:], wa_rows[:, :, P:])

        w2c = new_tile([P, 2 * H], U8, "w2c")
        w2s = new_tile([P, H], U8, "w2s")
        nc.scalar.copy(
            w2c[:, 0:H].bitcast(U32).rearrange("p (h q g) -> p h q g", h=2, g=2),
            w2raw[:].bitcast(U32).rearrange("p (h g q u) -> p h q g u", h=2, g=2, u=2)[:, :, :, :, 0],
        )
        nc.scalar.copy(
            w2s[:, 0 : H // 2].bitcast(U16).rearrange("p (h q g) -> p h q g", h=2, g=2),
            w2sraw[:].bitcast(U16).rearrange("p (h g q u) -> p h q g u", h=2, g=2, u=2)[:, :, :, :, 0],
        )
        w2half = w2raw[:].bitcast(U16).rearrange("p (g q t) -> p t q g", g=4, t=PACK)
        w2byte = w2sraw[:].rearrange("p (g q t) -> p t q g", g=4, t=PACK)
        nc.scalar.copy(w2c[:, H : H + 2 * P].bitcast(U16).rearrange("p (q g) -> p q g", g=4), w2half[:, 2])
        nc.scalar.copy(w2c[:, H + 2 * P :].bitcast(U16).rearrange("p (g q) -> p q g", g=4), w2half[:, 3])
        nc.gpsimd.tensor_copy(w2s[:, 2 * P : 3 * P].rearrange("p (q g) -> p q g", g=4), w2byte[:, 2])
        nc.gpsimd.tensor_copy(w2s[:, 3 * P :].rearrange("p (g q) -> p q g", g=4), w2byte[:, 3])

        page = [new_tile([P, T2], F32, f"page{t}") for t in range(PACK)]
        h1 = [new_tile([P, S], F32, f"h1_{t}") for t in range(PACK)]
        h2_tags = ["h2_0", "h2_1", "w1raw1", "w1b"]
        h2 = []

        def glossy(t):
            h2.append(new_tile([P, S], F32, f"h2_{t}", h2_tags[t]))
            linear = new_tile([P, S], F32, "linear")
            for b in range(2):
                cols = slice(BANK * b, BANK * (b + 1))
                acc = new_bank([P, BANK], (2 * t + b) % 4)
                nc.tensor.matmul_mx(
                    acc[:],
                    lhsT=w2c[:, 2 * P * t : 2 * P * (t + 1)].bitcast(FP4X4),
                    lhsT_scale=w2s[:, P * t : P * (t + 1)],
                    rhs=g2w[:, cols].bitcast(FP8X4),
                    rhs_scale=g2s[:, cols],
                    start=True, stop=True,
                )
                nc.scalar.activation(linear[:, cols], acc[:], ACT.Exp)
            for b in range(2):
                cols = slice(BANK * b, BANK * (b + 1))
                nc.scalar.activation(h2[t][:, cols], linear[:, cols], ACT.Copy, scale=tints[t][:])

        def scatter(t, places, h, wg):
            nc.vector.tensor_tensor(page[t][:].indirect(places[:]), h[t][:], wg[t][:], MULT)

        for t in range(2):
            glossy(t)
            scatter(t, o4, h2, wg2_sb)

        w1b = new_tile([P, 2, PACK, P, PACK], BF16, "w1b")
        for a in range(2):
            by_pair = w1raw[a][:].rearrange("p j (h g q t) -> p h q g t j", h=2, g=2, t=PACK)
            by_row = w1raw[a][:].rearrange("p j (g q t) -> p t q g j", g=4, t=PACK)
            for h in range(2):
                nc.scalar.copy(w1b[:, a, h].rearrange("p (q g e) j -> p q g e j", g=2, e=2), by_pair[:, h, :, :, 0:2, :])
            nc.scalar.copy(w1b[:, a, 2].rearrange("p (q g) j -> p q g j", g=4), by_row[:, 2])
            nc.scalar.copy(w1b[:, a, 3].rearrange("p (g q) j -> p q g j", g=4), by_row[:, 3])
        w1c = new_tile([P, PACK * 2 * P], U32, "w1c")
        w1s = new_tile([P, PACK * 2 * P], U8, "w1s")
        nc.vector.quantize_mx(w1c[:].bitcast(FP8X4), w1s[:], w1b[:].rearrange("p a t m j -> p (a t m j)"))

        glossy(2)
        scatter(2, o4, h2, wg2_sb)

        for t in (0, 2, 1, 3):
            for b in range(2):
                cols = slice(BANK * b, BANK * (b + 1))
                acc = new_bank([P, BANK], (2 * t + b) % 4)
                for a in range(2):
                    wcols = slice(P * (PACK * a + t), P * (PACK * a + t + 1))
                    nc.tensor.matmul_mx(
                        acc[:],
                        lhsT=w1c[:, wcols].bitcast(FP8X4),
                        lhsT_scale=w1s[:, wcols],
                        rhs=g1w[:, a, cols].bitcast(FP8X4),
                        rhs_scale=g1s[4 * a : P, cols],
                        start=(a == 0), stop=(a == 1),
                    )
                nc.scalar.activation(h1[t][:, cols], acc[:], ACT.Relu)

        glossy(3)
        warm = new_tile([P, 1], F32, "warm")
        nc.scalar.activation(warm[:], h2[PACK - 1][:, S - 1 : S], ACT.Sigmoid)

        for t in (0, 2, 1):
            scatter(t, o3, h1, wg1_sb)
        scatter(PACK - 1, o4, h2, wg2_sb)
        wac = new_tile([P, N], U32, "wac")
        was = new_tile([P, N], U8, "was")

        def quantise_wa(n):
            wab = new_tile([P, P, PACK], BF16, f"wab{n}")
            nc.scalar.copy(wab[:], waraw[n][:].rearrange("p j n -> p n j"))
            rows = slice(P * n, P * (n + 1))
            nc.vector.quantize_mx(wac[:, rows].bitcast(FP8X4), was[:, rows], wab[:].rearrange("p n j -> p (n j)"))

        quantise_wa(0)
        scatter(PACK - 1, o3, h1, wg1_sb)
        quantise_wa(1)

        on_vector = (0, 2)
        first, mid, second = 1, 2, 3
        ring = [0]

        def next_bank(shape):
            ring[0] = (ring[0] + 1) % 4
            return new_bank(shape, 4 + ring[0])

        def block(c, blk):
            return slice(BANK * c + P * blk, BANK * c + P * (blk + 1))

        def turned_sums(t, round_off):
            held = [new_bank([P, BLOCKS, P], c) for c in range(CHUNKS)]
            for c in range(CHUNKS):
                for blk in range(BLOCKS):
                    nc.tensor.matmul(held[c][:, blk, :], lhsT=hist_sb[t][:, block(c, blk)], rhs=ident[:], is_transpose=True, start=(blk == 0), stop=False)
            for c in range(CHUNKS):
                for blk in range(BLOCKS):
                    nc.tensor.matmul(held[c][:, blk, :], lhsT=page[t][:, block(c, blk)], rhs=ident[:], is_transpose=True, start=False, stop=(blk == BLOCKS - 1))
                round_off(t, c, held[c])

        def words(zt, blk):
            return zt[:].rearrange("m b p e -> m (b p e)").bitcast(F32)[:, P * blk : P * (blk + 1)]

        half = BANK // 2
        lead = 32
        give = 48
        pieces = ((0, 0, half), (mid, 0, half), (mid, half, BANK))
        pairs = [new_tile([P, 2, half + (lead if i == 2 else 0)], F32, f"pairs{i}") for i in range(len(pieces))]

        def turn_back(zt, u, c, bank):
            for i, (chunk, lo, hi) in enumerate(pieces):
                if chunk == c:
                    for at in range(lo, hi, P):
                        nc.tensor.transpose(bank[:, at : at + P], words(zt, at // P), ident[:])
            for i, (chunk, lo, hi) in enumerate(pieces):
                if chunk == c:
                    nc.scalar.copy(pairs[i][:, u, 0:half], bank[:, lo:hi])

        low = [new_tile([P, BLOCKS, P, 2], BF16, f"low{c}") for c in range(CHUNKS)]

        def round_pairs(t, c, bank):
            nc.scalar.copy(
                low[c][:, :, 64 * t : 64 * (t + 1), :].rearrange("m b (g q) e -> m b g q e", g=2),
                bank[:].rearrange("m b (q g e) -> m b g q e", g=2, e=2),
            )

        high_all = new_tile([P, CHUNKS, BLOCKS, P, 2], BF16, "high", "w1raw1")
        nc.gpsimd.memset(high_all[:].rearrange("m c b p e -> m (c b p e)").bitcast(I32), 0)
        high = [high_all[:, c] for c in range(CHUNKS)]

        def round_singles(t, c, bank):
            nc.scalar.copy(
                high[c][:, :, :, 0].rearrange("m b (g q) -> m b g q", g=4),
                bank[:].rearrange("m b (q g) -> m b g q", g=4),
            )

        hist_t = new_tile([P, CHUNKS, BANK], F32, "hist_t", "w1raw0")
        for c in on_vector:
            bank = next_bank([P, BLOCKS, P])
            for blk in range(BLOCKS):
                nc.tensor.transpose(bank[:, blk, :], hist_sb[PACK - 1][:, block(c, blk)], ident[:])
            nc.scalar.copy(hist_t[:, c, :], bank[:].rearrange("m b p -> m (b p)"))
        turned_sums(0, round_pairs)
        turned_sums(2, round_singles)
        for c in on_vector:
            turn_back(high[c], 1, c, next_bank([P, BANK]))
        turned_sums(1, round_pairs)
        for c in on_vector:
            turn_back(low[c], 0, c, new_bank([P, BANK], 4 + c // 2))

        late = new_tile([P, 2 * BANK, 2], F32, "late", "hist2")
        early = new_tile([P, 2 * BANK, 2], F32, "early", "tab2w")
        zb = [early[:, 0:BANK, :], early[:, BANK:, :], late[:, 0:BANK, :], late[:, BANK:, :]]

        for c, lo, index in ((0, half, 6), (second, 0, 7), (second, half, 0), (first, 0, 1), (first, half, 2)):
            bank = new_bank([P, 2, half], index)
            for u, zt in enumerate((low[c], high[c])):
                for at in range(0, half, P):
                    nc.tensor.transpose(bank[:, u, at : at + P], words(zt, (lo + at) // P), ident[:])
            skip = lead if (c, lo) == (second, 0) else 0
            if skip:
                nc.scalar.copy(pairs[2][:, :, half:], bank[:, :, 0:skip])
            nc.scalar.copy(zb[c][:, lo + skip : lo + half, :], bank[:, :, skip:].rearrange("p u m -> p m u"))
        hist_ps = {}
        for c, lo, hi, index in ((0, 0, P, 6), (0, P, half, 7), (mid, 0, BANK, 0), (0, half, BANK, 1)):
            bank = new_bank([P, hi - lo], index)
            for at in range(lo, hi, P):
                nc.tensor.transpose(bank[:, at - lo : at - lo + P], hist_t[:, c, at : at + P], ident[:])
            hist_ps[c, lo] = bank

        free_tags = ["h2_0", "h2_1", "linear", "wg1_pairs", "h1_0", "h1_1", "h1_2", "h1_3"]
        last = page[PACK - 1]
        by_half = out.rearrange("(n p) m -> p n m", n=2)

        def rounded(c):
            return zb[c].rearrange("p m u -> p (m u)").bitcast(BF16)

        def fourth(c):
            return rounded(c).rearrange("p (m j) -> p m j", j=PACK)[:, :, PACK - 1]

        def add_in_place(tile, base, lo, hi):
            dst = tile[:, lo - base : hi - base, :].rearrange("p m u -> p (m u)").bitcast(BF16).rearrange("p (m j) -> p m j", j=PACK)
            nc.gpsimd.tensor_tensor(dst[:, :, PACK - 1], last[:, lo:hi], hist_sb[PACK - 1][:, lo:hi], ADD)

        def add_to_pairs(i, lo, hi, held):
            c, base = pieces[i][0:2]
            halves = pairs[i][:, 1, lo - base : hi - base].bitcast(BF16).rearrange("p (m e) -> p m e", e=2)
            nc.vector.tensor_tensor(halves[:, :, 1], held, last[:, BANK * c + lo : BANK * c + hi], ADD)

        def quantise(c, lo, hi, tag=None):
            codes = new_tile([P, hi - lo], U32, f"zc{c}_{lo}", tag)
            scales = new_tile([P, hi - lo], U8, f"zs{c}_{lo}")
            nc.vector.quantize_mx(codes[:].bitcast(FP8X4), scales[:], rounded(c)[:, PACK * lo : PACK * hi])
            return codes, scales

        def passes(weights, index, z, halves):
            width = z[0].shape[1]
            acc = new_bank([P, len(halves), width], index)
            for i, n in enumerate(halves):
                rows = slice(P * n, P * (n + 1))
                nc.tensor.matmul_mx(
                    acc[:, i, :], lhsT=weights[0][:, rows].bitcast(FP8X4), lhsT_scale=weights[1][:, rows],
                    rhs=z[0][:].bitcast(FP8X4), rhs_scale=z[1][:], start=True, stop=True,
                )
            return acc

        vis_banks = ((3, 2), (4,), (5,), (2,), (3,), (4,), (5,), (2, 3))
        light_banks = (6, 0, 1, 7)
        gate_tags = {1: "late_a", 2: "late_b"}

        def gate_of(turn, z, halves, parts):
            vis = [passes((wbw, wbs), index, z, halves[part]) for index, part in zip(vis_banks[turn], parts)]
            gate = new_tile([P, len(halves), z[0].shape[1]], F32, f"gate{turn}", gate_tags.get(turn))
            for acc, part in zip(vis, parts):
                nc.scalar.activation(gate[:, part, :], acc[:], ACT.Sigmoid)
            return gate

        def multiply(turn, z, halves, parts):
            gate = gate_of(turn, z, halves, parts)
            return passes((wac, was), light_banks[turn % 4], z, halves), gate

        def read_out(turn, at, halves, parts, light, gate):
            res = new_tile(list(light.shape), F32, f"res{turn}", free_tags[turn])
            width = light.shape[2]
            dst = by_half[:, halves[0] : halves[-1] + 1, at : at + width]
            for part in parts:
                nc.vector.tensor_tensor(res[:, part, :], light[:, part, :], gate[:, part, :], MULT)
                nc.sync.dma_start(dst[:, part, :], res[:, part, :])

        both, whole, apart, one = (0, 1), (slice(0, 2),), (slice(0, 1), slice(1, 2)), (slice(0, 1),)
        add_in_place(early, 0, BANK - give, 2 * BANK)
        add_to_pairs(0, 0, P, hist_ps[0, 0][:])
        add_to_pairs(0, P, half, hist_ps[0, P][:])
        warm_bank = new_bank([P, BANK], 6)
        for k in range(3):
            nc.tensor.matmul_mx(
                warm_bank[:], lhsT=w2c[:, 0 : 2 * P].bitcast(FP4X4), lhsT_scale=w2s[:, 0:P],
                rhs=g2w[:, 0:BANK].bitcast(FP8X4), rhs_scale=g2s[:, 0:BANK], start=True, stop=True,
            )
        nc.scalar.copy(zb[0][:, 0:half, :], pairs[0][:].rearrange("p u m -> p m u"))
        add_to_pairs(1, 0, half, hist_ps[mid, 0][:, 0:half])
        add_to_pairs(2, half, BANK, hist_ps[mid, 0][:, half:])
        nc.vector.tensor_tensor(fourth(0)[:, half : BANK - give], hist_ps[0, half][:, 0 : half - give], last[:, half : BANK - give], ADD)
        nc.scalar.copy(late[:, 0:half, :], pairs[1][:].rearrange("p u m -> p m u"))
        nc.scalar.copy(late[:, half : BANK + lead, :], pairs[2][:].rearrange("p u m -> p m u"))
        z = [quantise(0, 0, half), quantise(0, half, BANK), quantise(first, 0, BANK), quantise(mid, 0, BANK)]
        add_in_place(late, 2 * BANK, 3 * BANK, T2)
        turns = [
            (z[0], 0, both, apart, whole), (z[1], half, both, whole, whole),
            (z[2], BANK * first, (0,), one, one), (z[2], BANK * first, (1,), one, one),
            (z[3], BANK * mid, (0,), one, one), (z[3], BANK * mid, (1,), one, one),
        ]
        gates = [gate_of(turn, turns[turn][0], turns[turn][2], turns[turn][3]) for turn in range(2)]
        ready = [(passes((wac, was), light_banks[turn], turns[turn][0], both), gates[turn]) for turn in range(2)]
        ready.extend(multiply(turn, turns[turn][0], turns[turn][2], turns[turn][3]) for turn in (2, 3))
        for turn in range(4):
            read_out(turn, turns[turn][1], turns[turn][2], turns[turn][4], *ready[turn])
            if turn < 2:
                ready.append(multiply(turn + 4, turns[turn + 4][0], turns[turn + 4][2], turns[turn + 4][3]))
        for turn in range(4, 8):
            if turn < 6:
                lo = half * (turn - 4)
                parts = apart if lo else whole
                turns.append((quantise(second, lo, lo + half, gate_tags[turn - 3]), BANK * second + lo, both, parts, parts))
                ready.append(multiply(turn + 2, turns[turn + 2][0], both, parts))
            read_out(turn, turns[turn][1], turns[turn][2], turns[turn][4], *ready[turn])
